import numpy as np, ml_dtypes
CORES = [10,34,74,98]
N = 4
import mx_ref
BF = ml_dtypes.bfloat16
def gentries(a):
    return np.ascontiguousarray(a.reshape(8, 16, -1).transpose(0, 2, 1)).reshape(8, -1)
def gtable(e):
    e = np.asarray(e); return np.ascontiguousarray(e.reshape(8, -1, 16).transpose(0, 2, 1)).reshape(128, -1).astype(np.int32)
def gcols(t, e):
    v = np.concatenate([t.reshape(8, 16, -1, 4), np.zeros((8, 16, 1, 4), BF)], axis=2)
    return np.ascontiguousarray(np.stack([v[g][:, e[g]] for g in range(8)])).reshape(128, -1)
def tile(rs):
    return np.stack(rs, axis=2).reshape(128, -1).astype(BF)
def pick(q, e):
    c = np.concatenate([q[0].reshape(128, -1, 4), np.zeros((128, 1, 4), np.uint8)], axis=1); s = np.concatenate([q[1], np.ones((16, 1), np.uint8)], axis=1)
    return (np.ascontiguousarray(c[:, e].reshape(128, -1)), np.ascontiguousarray(s[:, e]))
def join(*qs):
    return (np.concatenate([q[0] for q in qs], axis=1), np.concatenate([q[1] for q in qs], axis=1))
def put(q, e, v):
    c, s = q[0].reshape(128, -1, 4).copy(), q[1].copy(); c[:, e] = v[0].reshape(128, -1, 4); s[:, e] = v[1]
    return (c.reshape(128, -1), s)
def pk(c, s):
    return (np.ascontiguousarray(c), mx_ref.live(s))
def emit(q):
    return q[0], q[1]
def packed(v, rng):
    q = [mx_ref.quantize(np.ascontiguousarray(v[r])) for r in range(N)]
    return np.stack([a for a, b in q]), np.stack([mx_ref.plane(b, rng) for a, b in q])
def values_of_codes():
    e, c = np.zeros((128, 128, 4), np.float32), np.zeros((128, 2, 4), np.uint8)
    e[np.arange(128), np.arange(128), 0] = 1
    c[:127, :, 0] = np.arange(256).reshape(2, 128).T[:127]
    return mx_ref.matmul(mx_ref.quantize(e.reshape(128, 512).astype(BF)), (c.reshape(128, 8), np.full((16, 2), 127, np.uint8))).T.reshape(-1).astype(np.float64)
CODE_VALUE, SCALE_VALUE = values_of_codes(), 2.0 ** (np.arange(256) - 127.0)
def decode(q):
    return (CODE_VALUE[q[0]].reshape(16, 8, -1, 4) * SCALE_VALUE[q[1]][:, None, :, None] + 0.0).reshape(128, -1).astype(np.float32)
def f(rng, *shape):
    return mx_ref.flush((rng.standard_normal(shape, dtype=np.float32) * np.exp2(rng.integers(-2, 3, shape[:-1] + (1,)))).astype(BF))
def wide(rng, *shape, cols=0):
    v = rng.standard_normal(shape, dtype=np.float32) * np.exp2(rng.integers(-12, 13, shape)).astype(np.float32)
    if cols: v *= np.repeat(np.exp2(rng.integers(-cols, cols + 1, shape[:-2] + (1, shape[-1] // 4))) * (rng.random(shape[:-2] + (1, shape[-1] // 4)) > 0.0625), 4, axis=-1).astype(np.float32)
    return mx_ref.flush(v.astype(BF))
C, HALF, E = 320, 160, 256
MASK = [1, 2, 3]
TIMES = 9
def register(b):
    a = 2 * np.arange(HALF)
    return np.concatenate([a + b, a + 1 - b], axis=-1)
def lowest(s):
    low, to = np.broadcast_to(np.arange(C), s.shape), s
    for i in range(TIMES):
        low = np.minimum(low, np.take_along_axis(low, to, axis=-1))
        to = np.take_along_axis(to, to, axis=-1)
    return low
def joined(s):
    low, c = lowest(s), np.arange(HALF)
    a, b = low[..., :HALF], low[..., HALF:]
    swap = (a != b) & ((a == c) & (c > 0) | (b == c + HALF))
    return np.concatenate([np.where(swap, s[..., HALF:], s[..., :HALF]), np.where(swap, s[..., :HALF], s[..., HALF:])], axis=-1)
def numbers_of(rng):
    return {"x": np.array(f(rng, N, 128, 4 * C)), "u": np.array(f(rng, N, 128, 512)), "v": np.array(f(rng, N, 128, 512))}
def orders(rng):
    return rng.permuted(np.tile(np.arange(C), (N, 8, 1)), axis=2)
def stored(k):
    return {"kl": np.stack([gtable(k[r]) for r in range(N)])}
def layers(rng):
    return np.array(f(rng, N, 128, 2048)).reshape(N, 8, 16, 4, 8, 16, 4)
def weights(rng, w):
    c, p = packed(np.ascontiguousarray(w).reshape(N, 128, 2048), rng)
    return {"wc": c, "ws": p}
def setup_inputs(rng):
    return {**numbers_of(rng), **stored(orders(rng)), **weights(rng, layers(rng))}
def setup_inputs_ties(rng):
    d = numbers_of(rng)
    o = rng.permutation(N)
    k = rng.integers(-1, 2, (N, 8, C)).astype(np.float32)
    k[o[1]] = 1
    x = d["x"].reshape(N, 8, 16, C, 4)
    x[:, :, 0] = 0
    x[:, :, 0, :, 0] = k.astype(BF)
    a = np.exp2(rng.integers(-3, 4, (8, 1)).astype(np.float64))
    j = rng.integers(3, 7, (8, 4, 6))
    j[:, :, 0] = 6
    q = (9 + 2 * rng.integers(0, 4, (8, 4, 6))) * 0.125 * np.exp2(-j.astype(np.float64))
    x[:, :, 8:] = 0
    x[:, :, 8, :, 0] = (-3.0 * a).astype(np.float32).astype(BF)
    x[:, :, 10, :, 0] = (-0.140625 * a).astype(np.float32).astype(BF)
    x[:, :, 10, :, 1] = (-0.125 * a).astype(np.float32).astype(BF)
    c = np.ones(N, np.float32)
    c[o[0]] = 0
    c[o[2]] = -1
    u = d["u"].reshape(N, 128, 128, 4)
    u[:, :, ::16] = 0
    for h in range(0, 128, 16): u[:, h, h, 0] = c.astype(BF)
    w = layers(rng)
    w[:, :, 0] = 0
    w[:, :, :, :, :, 0] = 0
    w[:, :, :, :, :, 8:] = 0
    for g in range(8): w[:, g, 10, 0, g, 8, 0] = -224.0
    for n, i in enumerate((9, 11, 12, 13, 14, 15)):
        x[:, :, i] = (q[:, :, n] * a * -0.0078125)[:, None].astype(np.float32).astype(BF)
        for g in range(8): w[:, g, 10, :, g, i, 1] = (-q[g, :, n]).astype(np.float32).astype(BF)
    return {"x": x.reshape(N, 128, 4 * C), "u": u.reshape(N, 128, 512), "v": d["v"], **stored(orders(rng)), **weights(rng, w)}
def setup_inputs_near(rng):
    d = numbers_of(rng)
    o = rng.permutation(N) % 4
    k = np.where((o == 1) | (o == 2), 1.0, 2.0 ** -30).astype(np.float32)
    x = d["x"].astype(np.float32).reshape(N, 8, 16, C, 4)
    x[:, :, :8] = 0
    s = rng.integers(-1, 2, (N, 8, C)) * k[:, None, None]
    s[o == 3] = 0
    x[:, :, 0, :, 0] = 1.125 * s
    x[:, :, 1, :, 0] = -1.25 * s
    x[:, :, 7, :, 0] = 2.0 ** -30
    w = layers(rng)
    w[:, :, :8] = 0
    w[:, :, :, :, :, :8] = 0
    for r in range(N):
        if o[r] == 3:
            x[r, :, 4, :, 0] = rng.choice([-1.0, 1.0], (8, C)) * 2.0 ** -30
            for g in range(8):
                w[r, g, 4, 0, g, 0, 0] = 1.125 * 2.0 ** -8
                w[r, g, 4, 0, g, 1, 0] = -1.25 * 2.0 ** -8
                w[r, g, 7, 0, g, 6, 0] = 2.0 ** 5
        at = [0, C - 1, int(rng.integers(C)), int(rng.integers(C))]
        for g, j in zip(rng.permutation(8)[:4], at): x[r, g, 0, j, 0] = 2.0 ** 30 * rng.choice([-1.0, 1.0])
    u = d["u"].reshape(N, 128, 128, 4)
    u[:, :, ::16] = 0
    for h in range(0, 128, 16):
        u[:, h, h, 0] = (1.125 * k).astype(np.float32).astype(BF)
        u[:, h + 1, h, 0] = k.astype(BF)
    return {"x": x.reshape(N, 128, 4 * C).astype(BF), "u": u.reshape(N, 128, 512), "v": d["v"], **stored(orders(rng)), **weights(rng, w)}
def setup_inputs_long(rng):
    d = numbers_of(rng)
    k = orders(rng)
    b = rng.integers(0, 2, (N, 8, HALF))
    for c in rng.permutation(HALF):
        low = lowest(register(b))
        b[..., c] ^= (low[..., c] != low[..., c + HALF]).astype(np.int64)
    last = HALF - 1 - (HALF - 1) // 2
    way = [last >> i for i in range(last.bit_length() - 1, -1, -1)]
    for r in range(N):
        t = rng.permutation(8)
        for g in t[2:4]: b[r, g, rng.integers(1, HALF)] ^= 1
        b[r, t[4], 0] ^= 1
        for g in t[5:]: b[r, g] = rng.integers(0, 2, HALF)
        for g in t[5:7]:
            b[r, g, HALF - 1] = 0
            for i, j in zip(way, way[1:]): b[r, g, HALF - 1 - i] = j & 1
            b[r, g, HALF - 1 - last] = 1 - (HALF - 1) % 2
    s = np.zeros((N, 8, C))
    np.put_along_axis(s, k, np.concatenate([b, rng.integers(0, 2, (N, 8, HALF))], axis=2) * 2.0 - 1.0, axis=2)
    x = d["x"].reshape(N, 8, 16, C, 4)
    x[:, :, 0] = 0
    x[:, :, 0, :, 0] = (s * np.exp2(rng.integers(-3, 4, (N, 8, C)).astype(np.float64))).astype(np.float32).astype(BF)
    u = d["u"].reshape(N, 128, 128, 4)
    u[:, :, ::16] = 0
    for h in range(0, 128, 16): u[:, h, h, 0] = 1
    w = layers(rng)
    w[:, :, :, :, :, 0] = (w[:, :, :, :, :, 0].astype(np.float32) * 4).astype(BF)
    return {"x": x.reshape(N, 128, 4 * C), "u": u.reshape(N, 128, 512), "v": d["v"], **stored(k), **weights(rng, w)}
def setup_inputs_ends(rng):
    d = numbers_of(rng)
    o, e = rng.permutation(N) % 4, rng.permutation(N) % 4
    k = orders(rng)
    x = np.zeros((N, 8, 16, C, 4))
    u = d["u"].astype(np.float32).reshape(N, 128, 128, 4)
    v = np.zeros((N, 128, 512))
    w = np.zeros((N, 128, 4, 128, 4), np.float32)
    i = np.arange(128)[np.arange(128) % 16 < 15]
    j = np.arange(14, 128, 16)
    up, down = np.arange(C), np.arange(C)[::-1]
    for r in range(N):
        if e[r] == 0: k[r] = up
        if e[r] == 1: k[r] = down
        if e[r] == 2: k[r] = np.where(rng.permutation(8)[:, None] < 4, up, down)
        h = rng.permutation(8)
        c = np.where(h < 2, 0.0, h % 2 * 2.0 - 1.0)[None, :, None]
        much = (0.9 + 0.1 * rng.random((8, 16, C, 4))) * 2.0 ** 29
        if o[r] == 0: x[r] = -much
        if o[r] == 1: x[r] = much * rng.choice([-1.0, 1.0], (1, 1, C, 1))
        if o[r] == 2: x[r] = -(1.0 + 0.125 * rng.integers(0, 8, (8, 16, C, 4))) * 2.0 ** -30
        if o[r] == 3: x[r] = d["x"][r].astype(np.float32).reshape(8, 16, C, 4)[:, :, :1]
        x[r, :, 15] = 2.0 ** -30
        if o[r] < 2:
            u[r, :, ::16] = c * (0.9 + 0.1 * rng.random((128, 8, 4))) * 2.0 ** 30
            v[r] = (0.9 + 0.1 * rng.random((128, 512))) * 2.0 ** 30
        else:
            v[r] = (1.0 + 0.125 * rng.integers(0, 8, (128, 512))) * 2.0 ** -30
        if o[r] == 2: u[r, :, ::16] = c * (1.0 + 0.125 * rng.integers(0, 8, (128, 8, 4))) * 2.0 ** -30
        if o[r] == 3: u[r, :, ::16] *= np.abs(c).astype(np.float32)
        n = np.array([1.0, 2.0, 4.0])[rng.permutation(8) % 3]
        for b in range(4):
            if o[r] != 2: w[r, i, b, i, b] = -n[i // 16]
            else:
                w[r, i, b, i, b] = -2.0 ** -8
                w[r, j, b, j, b] = 0.0
                w[r, j + 1, b, j, b] = 2.0 ** 8
                w[r, j - 8, b, j - 8, b] = 0.0
                w[r, j + 1, b, j - 8, b] = 2.0 ** 5
    v = v * rng.choice([-1.0, 1.0], (N, 128, 512))
    return {"x": x.astype(np.float32).reshape(N, 128, 4 * C).astype(BF), "u": u.reshape(N, 128, 512).astype(BF), "v": v.astype(np.float32).astype(BF), **stored(k), **weights(rng, w.astype(BF))}
def setup_inputs_spread(rng):
    d = setup_inputs(rng)
    d["x"] = wide(rng, N, 128, 4 * C, cols=6)
    return d
def check_inputs(d):
    b = []
    for k in ("x", "u", "v"):
        a = np.abs(d[k].astype(np.float32))
        if not (np.isfinite(a).all() and ((a == 0) | (a >= 2.0 ** -30) & (a <= 2.0 ** 30)).all()): b.append("a value of " + k)
    none, least, most = [emit(mx_ref.quantize(np.full((128, 16), k, np.float32).astype(BF)))[1][0, 0] for k in (0.0, 2.0 ** -8, 2.0 ** 8)]
    for r in range(N):
        if not (np.sort(gentries(d["kl"][r]), axis=1) == np.arange(C)).all(): b.append("kl: not a permutation")
        if ((d["wc"][r] == 0x7F) | (d["wc"][r] == 0xFF)).any(): b.append("wc: a code that is no number")
        s = mx_ref.live(d["ws"][r])
        if ((s != none) & ((s < least) | (s > most))).any(): b.append("ws: a scale out of range")
    return b
def reference(x, u, v, kl, wc, ws):
    qu = [mx_ref.quantize(u[r]) for r in range(N)]
    lay = [pk(wc[r], ws[r]) for r in range(N)]
    now = [x[r] for r in range(N)]
    k = [gentries(kl[r]).astype(np.int64) for r in range(N)]
    for m in MASK:
        e, made = [], []
        for r in range(N):
            s = mx_ref.matmul(qu[r], mx_ref.quantize(now[r]))[::16]
            bits = (np.take_along_axis(s, k[r][:, :HALF], axis=1) > 0).astype(np.int64)
            e.append(np.take_along_axis(k[r], joined(register(bits)), axis=1))
            z = (gcols(now[r], k[r]).astype(np.float32) + gcols(now[r], e[r]).astype(np.float32)) * np.float32(0.5)
            q = mx_ref.quantize(z.astype(BF))
            made.append(tile([mx_ref.matmul(pick(lay[r], np.arange(128 * b, 128 * b + 128)), q) * np.float32(0.03125) for b in range(4)]))
        k = [np.take_along_axis(k[r ^ m], e[r], axis=1) for r in range(N)]
        for r in range(N):
            far = decode(mx_ref.quantize(np.ascontiguousarray(made[r ^ m][:, :4 * E]))).astype(BF)
            both = np.concatenate([far, made[r][:, 4 * E:]], axis=1)
            now[r] = (now[r].astype(np.float32) + gcols(both, k[r]).astype(np.float32)).astype(BF)
    y, kp = np.zeros((N, 128, C), np.float32), np.zeros((N, 8, C), np.float32)
    oc, osc = np.zeros((N, 128, 4 * C), np.uint8), np.zeros((N, 16, C), np.uint8)
    for r in range(N):
        q = mx_ref.quantize(now[r])
        y[r] = mx_ref.matmul(mx_ref.quantize(v[r]), q)
        kp[r] = k[r]
        oc[r], osc[r] = emit(q)
    return {"y": y, "kp": kp, "oc": oc, "osc": osc}

@@ -1,0 +1,405 @@
+from concourse.mybir import dt, AluOpType, ActivationFunctionType
+
+C, HALF, CROSS = 320, 160, 256
+ROUNDS = 3
+MASKS = [1, 2, 3]
+RADIX = [3, 3, 3, 3, 4]
+BIG = 1024.0
+F32, BF, I32, U16, F8, U8 = "float32", "bfloat16", "int32", "uint16", "float8_e4m3fn_x4", "uint8"
+
+SCRATCH = {
+    "ub": ("sbuf", [128, 512], BF), "vb": ("sbuf", [128, 512], BF),
+    "uq": ("sbuf", [128, 128], F8), "us": ("sbuf", [128, 128], U8),
+    "vq": ("sbuf", [128, 128], F8), "vs": ("sbuf", [128, 128], U8),
+    "wq": ("sbuf", [128, 512], F8), "wp": ("sbuf", [128, 512], U8),
+    "one": ("sbuf", [128, 512], BF), "eb": ("sbuf", [128, 2048], BF),
+    "eq": ("sbuf", [128, 512], F8), "ep": ("sbuf", [128, 512], U8),
+    "pidx": ("sbuf", [128, 1], I32), "qidx": ("sbuf", [128, 1], I32), "grp": ("sbuf", [128, 1], I32), "par": ("sbuf", [128, 1], I32),
+    "yrow": ("sbuf", [128, C], F32), "cwi": ("sbuf", [128, 16], F32), "cst": ("sbuf", [128, 16], F32), "sel": ("sbuf", [128, 8], U16),
+    "k1": ("sbuf", [128, HALF], BF), "k3": ("sbuf", [128, HALF], F32), "bs0": ("sbuf", [128, C], BF),
+    "cw": ("sbuf", [128, 16], F32), "ca": ("sbuf", [128, 16], F32), "cb": ("sbuf", [128, 16], F32), "cd": ("sbuf", [128, 16], F32),
+    "ct0": ("sbuf", [128, 16], F32), "ct1": ("sbuf", [128, 16], F32),
+    "dl": ("sbuf", [128, 64], F32), "dat": ("sbuf", [128, 64], F32), "sc": ("sbuf", [128, 64], F32), "sd": ("sbuf", [128, 16], F32),
+    "kli": ("sbuf", [128, 20], I32), "klb": ("sbuf", [128, 32], BF), "klt": ("sbuf", [128, 32], BF),
+    "gg": ("sbuf", [128, 5 * 352], BF), "krs": ("sbuf", [128, 3 * C], BF),
+    "bits": ("sbuf", [128, C], BF), "bs1": ("sbuf", [128, C], BF), "bs2": ("sbuf", [128, C], BF),
+    "tt": ("sbuf", [128, 672], BF), "of0": ("sbuf", [128, 32], U16), "of1": ("sbuf", [128, 32], U16),
+    "kpf": ("sbuf", [128, C], F32), "yo": ("sbuf", [128, C], F32),
+    "ps": ("psum", [128, 4096], F32),
+}
+for _r in range(ROUNDS + 1):
+    SCRATCH["xt%d" % _r] = ("sbuf", [128, 4 * C], BF)
+    SCRATCH["xq%d" % _r] = ("sbuf", [128, C], F8)
+    SCRATCH["xs%d" % _r] = ("sbuf", [128, C], U8)
+    SCRATCH["kof%d" % _r] = ("sbuf", [128, 32], U16)
+for _r in range(ROUNDS):
+    SCRATCH["k4%d" % _r] = ("sbuf", [128, 128], U16)
+    SCRATCH["tof%d" % _r] = ("sbuf", [128, 20], U16)
+    SCRATCH["kk%d" % _r] = ("sbuf", [128, C], BF)
+    SCRATCH["yp%d" % _r] = ("sbuf", [128, 4 * C], BF)
+    SCRATCH["yi%d" % _r] = ("sbuf", [128, 4 * C], BF)
+    SCRATCH["zt%d" % _r] = ("sbuf", [128, 4 * C], BF)
+    SCRATCH["zq%d" % _r] = ("sbuf", [128, 384], F8)
+    SCRATCH["zs%d" % _r] = ("sbuf", [128, 384], U8)
+    SCRATCH["ht%d" % _r] = ("sbuf", [128, 4 * CROSS], BF)
+    SCRATCH["hq%d" % _r] = ("sbuf", [128, CROSS], F8)
+    SCRATCH["hs%d" % _r] = ("sbuf", [128, CROSS], U8)
+    SCRATCH["rq%d" % _r] = ("sbuf", [128, CROSS], F8)
+    SCRATCH["rs%d" % _r] = ("sbuf", [128, CROSS], U8)
+    SCRATCH["bp%d" % _r] = ("sbuf", [128, 4 * C], BF)
+    SCRATCH["lk%d" % _r] = ("dram", [128, 20], BF)
+    SCRATCH["rk%d" % _r] = ("dram", [128, 20], BF)
+SEMAPHORES = ["sv", "sa", "sp", "sg", "sent", "lx0", "lx1", "lu", "lv", "lk", "lwc", "lws",
+              "oc0", "oc1", "os", "oy0", "oy1", "okp"]
+for _r in range(ROUNDS):
+    SEMAPHORES += ["dk%d" % _r, "dr%d" % _r, "arl%d" % _r, "ar0%d" % _r, "ar1%d" % _r]
+
+
+def rank_program(g, core, T, topo):
+    rank = T.rank_of(core)
+    if rank is None:
+        return
+    A, ACT = AluOpType, ActivationFunctionType
+    queue = {"v": g.vector, "a": g.scalar, "p": g.tensor, "g": g, "s": g.sync}
+    own = {"v": "sv", "a": "sa", "p": "sp", "g": "sg"}
+    total, seen, hist = {}, {q: {} for q in queue}, {}
+
+    def need(q, reads, writes, compute):
+        deps = {}
+        for (names, isw) in ((reads, False), (writes, True)):
+            for (b, lo, hi) in names:
+                for (l, h, w, eq, sem, val) in hist.get(b, []):
+                    if l < hi and lo < h and (w or isw):
+                        if compute and eq == q and isw:
+                            continue
+                        deps[sem] = max(deps.get(sem, 0), val)
+        for sem in deps:
+            if seen[q].get(sem, 0) < deps[sem]:
+                queue[q].wait_ge(T.sem[sem], deps[sem])
+                seen[q][sem] = deps[sem]
+
+    def note(q, reads, writes, sem, val):
+        for (b, lo, hi) in writes:
+            hist[b] = [e for e in hist.get(b, []) if not (lo <= e[0] and e[1] <= hi and (e[3] != q or e[2] is False or (lo, hi) == (e[0], e[1])))]
+            hist[b].append((lo, hi, True, q, sem, val))
+        for (b, lo, hi) in reads:
+            keep = [e for e in hist.get(b, []) if not (not e[2] and e[3] == q and lo <= e[0] and e[1] <= hi)]
+            keep.append((lo, hi, False, q, sem, val))
+            hist[b] = keep
+
+    def op(q, call, reads, writes):
+        need(q, reads, writes, True)
+        sem = own[q]
+        total[sem] = total.get(sem, 0) + 1
+        call(queue[q]).then_inc(T.sem[sem], 1)
+        note(q, reads, writes, sem, total[sem])
+
+    def dma(q, sem, pairs):
+        for (out, in_, reads, writes) in pairs:
+            need(q, reads, writes, False)
+        for (out, in_, reads, writes) in pairs:
+            total[sem] = total.get(sem, 0) + 16
+            queue[q].dma_start(out, in_).then_inc(T.sem[sem], 16)
+        for (out, in_, reads, writes) in pairs:
+            note("d" + q, reads, writes, sem, total[sem])
+
+    def send(dst, out, in_, reads, sem):
+        need("g", reads, [], False)
+        rid, pid = topo.addr(dst)[0], topo.addr(dst)[1]
+        n = len(topo.engines(core, dst))
+        g.remote_dma(out, in_, T.sem[sem], T.sem.sent, pid, rid, topo.mask(core, dst))
+        total["sent"] = total.get("sent", 0) + n
+        total[sem] = total.get(sem, 0) + n
+
+    def tts(out, in0, s1, s2, o0, o1, reads, writes):
+        if o1 is None:
+            op("v", lambda e: e.tensor_scalar(out, in0, s1, None, o0), reads, writes)
+        else:
+            op("v", lambda e: e.tensor_scalar(out, in0, s1, s2, o0, o1), reads, writes)
+
+    def ttt(out, in0, in1, o, reads, writes):
+        op("v", lambda e: e.tensor_tensor(out, in0, in1, o), reads, writes)
+
+    def quant(q, s, a, b, t, ta, tb):
+        op("v", lambda e: e.quantize_mx(T[q][:, a:b], T[s][:, a:b], T[t][:, ta:tb]), [(t, ta, tb)], [(q, a, b), (s, a, b)])
+
+    def bank(i):
+        return ("ps", 512 * i, 512 * i + 512)
+
+    def mul(i, n, lq, ls, l, rq, rs, a, b):
+        op("p", lambda e: e.matmul_mx(T.ps[:, 512 * i:512 * i + n], T[lq][:, l:l + 128], T[ls][:, l:l + 128],
+                                      T[rq][:, a:b], T[rs][:, a:b], True, True),
+           [(lq, l, l + 128), (ls, l, l + 128), (rq, a, b), (rs, a, b)], [bank(i)])
+
+    peer = [T.cores[rank ^ m] for m in MASKS]
+    dma("s", "lx0", [(T.xt0[:, 0:512], T.x[:, 0:512], [], [("xt0", 0, 512)])])
+    dma("a", "lk", [(T.kli[:], T.kl[:, :], [], [("kli", 0, 20)])])
+    dma("s", "lx1", [(T.xt0[:, 512:1280], T.x[:, 512:1280], [], [("xt0", 512, 1280)])])
+    dma("a", "lu", [(T.ub[:], T.u[:, :], [], [("ub", 0, 512)])])
+    dma("s", "lwc", [(T.wq[:, 0:512].bitcast(dt.uint8), T.wc[:, 0:2048], [], [("wq", 0, 512)])])
+    dma("s", "lws", [(T.wp[:, 0:512], T.ws[:, 0:512], [], [("wp", 0, 512)])])
+    dma("a", "lv", [(T.vb[:], T.v[:, :], [], [("vb", 0, 512)])])
+
+    op("g", lambda e: e.iota(T.pidx[:], [[0, 1]], 0, 1), [], [("pidx", 0, 1)])
+    op("g", lambda e: e.iota(T.yrow[:], [[1, C]], 0, 0, allow_small_or_imprecise_dtypes=True), [], [("yrow", 0, C)])
+    op("g", lambda e: e.iota(T.cwi[:], [[16, 16]], 0, 1, allow_small_or_imprecise_dtypes=True), [], [("cwi", 0, 16)])
+    op("v", lambda e: e.memset(T.klb[:], 0.0), [], [("klb", 0, 32)])
+    op("v", lambda e: e.memset(T.one[:], 1.0), [], [("one", 0, 512)])
+    op("v", lambda e: e.memset(T.dl[:, 0:64:4], 0.0), [], [("dl", 0, 64)])
+    op("v", lambda e: e.memset(T.dl[:, 3:64:4], -1.0), [], [("dl", 0, 64)])
+
+    def col(i):
+        return T.cst[:, i:i + 1]
+
+    def cc(*i):
+        return [("cst", j, j + 1) for j in i]
+
+    def scol(i, in0, names, s1, s2, o0, o1):
+        tts(col(i), in0, s1, s2, o0, o1, names, cc(i))
+    P1, Q1, G1, PA = ("pidx", 0, 1), ("qidx", 0, 1), ("grp", 0, 1), ("par", 0, 1)
+    tts(T.qidx[:], T.pidx[:], 15, None, A.bitwise_and, None, [P1], [Q1])
+    tts(T.grp[:], T.pidx[:], 4, None, A.arith_shift_right, None, [P1], [G1])
+    scol(0, T.qidx[:], [Q1], 0.0, None, A.is_equal, None)
+    scol(1, T.qidx[:], [Q1], 0.0, BIG, A.is_equal, A.mult)
+    ttt(T.par[:], T.pidx[:], T.grp[:], A.add, [P1, G1], [PA])
+    scol(12, T.qidx[:], [Q1], 16.0, None, A.mult, None)
+    scol(8, T.grp[:], [G1], 16.0, None, A.mult, None)
+    scol(5, col(0), cc(0), 2.0, 2.0, A.mult, A.add)
+    scol(6, col(0), cc(0), -479.0, 160.0, A.mult, A.add)
+    tts(T.par[:], T.par[:], 1, None, A.bitwise_and, None, [PA], [PA])
+    scol(7, col(0), cc(0), -160.0, None, A.mult, None)
+    scol(4, col(0), cc(0), 1.0, None, A.add, None)
+    scol(10, T.qidx[:], [Q1], 4.0, 256.0, A.is_lt, A.mult)
+    scol(11, T.qidx[:], [Q1], 10.0, 160.0, A.is_lt, A.mult)
+    scol(9, T.par[:], [PA] + cc(12), 336.0, col(12), A.mult, A.add)
+    tts(T.cw[:], T.cwi[:], col(8), None, A.subtract, None, [("cwi", 0, 16)] + cc(8), [("cw", 0, 16)])
+
+    def widen(nm, n, scale, bias, names):
+        op("a", lambda e: e.activation(T[nm][:, 0:n], T.yrow[:, 0:n], ACT.Identity, bias=bias, scale=scale),
+           [("yrow", 0, C)] + names, [(nm, 0, n)])
+    widen("k1", HALF, col(4), col(7), cc(4, 7))
+    widen("k3", HALF, col(5), col(6), cc(5, 6))
+    widen("bs0", C, 1.0, col(1), cc(1))
+
+    def blank(nm, a, b):
+        op("a", lambda e: e.activation(T[nm][:, a:b], T.yrow[:, 0:b - a], ACT.Copy, scale=0.0), [("yrow", 0, C)], [(nm, a, b)])
+    for a, b in ((0, 16), (336, 368), (688, 720), (1040, 1072), (1392, 1424), (1744, 1760)):
+        blank("gg", a, b)
+    for i in range(ROUNDS):
+        blank("krs", C * i, C * i + C)
+    for c, i, row in ((0, None, 0), (1, 10, 0), (2, None, 1), (4, 11, 1)):
+        if i is None:
+            tts(T.sel[:, c:c + 1], col(9), float(row), None, A.add, None, cc(9), [("sel", c, c + 1)])
+        else:
+            tts(T.sel[:, c:c + 1], col(9), float(row), col(i), A.add, A.add, cc(9, i), [("sel", c, c + 1)])
+    CW = [("cw", 0, 16)]
+    tts(T.ca[:], T.cw[:], 0.0, None, A.is_equal, None, CW, [("ca", 0, 16)])
+    tts(T.cb[:], T.cw[:], 159.0, -160.0, A.is_equal, A.mult, CW, [("cb", 0, 16)])
+    tts(T.cd[:], T.cw[:], 159.0, 161.0, A.is_equal, A.mult, CW, [("cd", 0, 16)])
+    tts(T.dl[:, 1:64:4], T.cw[:], 159.0, 2.0, A.is_equal, A.mult, CW, [("dl", 0, 64)])
+    tts(T.dat[:, 3:64:4], T.cw[:], 4.0, -319.0, A.mult, A.add, CW, [("dat", 0, 64)])
+    ttt(T.ca[:], T.cw[:], T.ca[:], A.subtract, CW + [("ca", 0, 16)], [("ca", 0, 16)])
+    tts(T.dl[:, 1:64:4], T.dl[:, 1:64:4], -1.0, None, A.add, None, [("dl", 0, 64)], [("dl", 0, 64)])
+    ttt(T.ct0[:], T.ca[:], T.cb[:], A.add, [("ca", 0, 16), ("cb", 0, 16)], [("ct0", 0, 16)])
+    ttt(T.ct1[:], T.ca[:], T.cd[:], A.add, [("ca", 0, 16), ("cd", 0, 16)], [("ct1", 0, 16)])
+
+    KL = [("kli", 0, 20)]
+    tts(T.klb[:, 0:20], T.kli[:], -160.0, None, A.add, None, KL, [("klb", 0, 20)])
+    tts(T.kof0[:, 0:20], T.kli[:], 0.0, None, A.add, None, KL, [("kof0", 0, 20)])
+    op("v", lambda e: e.transpose(T.klt[:], T.klb[:]), [("klb", 0, 32)], [("klt", 0, 32)])
+    for t in range(4):
+        tts(T.k40[:, 32 * t:32 * t + 20], T.kli[:], 4.0, float(t), A.mult, A.add, KL, [("k40", 32 * t, 32 * t + 20)])
+    dma("s", "dk0", [(T.lk0[16 * i:16 * i + 16, :], T.klt[32 * (i // 2):32 * (i // 2) + 20, 16 * (i % 2):16 * (i % 2) + 16],
+                      [("klt", 0, 32)], [("lk0", 20 * i, 20 * i + 20)]) for i in range(8)])
+
+    def share(r):
+        send(peer[r], T["rk%d" % r][:, :], T["lk%d" % r][:, :], [("lk%d" % r, 0, 160)], "arl%d" % r)
+        note("net", [], [("rk%d" % r, 0, 160)], "arl%d" % r, total["arl%d" % r])
+        dma("s", "dr%d" % r, [(T.krs[0:128:16, C * r:C * r + C], T["rk%d" % r][:, :],
+                               [("rk%d" % r, 0, 160)], [("krs", C * r, C * r + C)])])
+
+    share(0)
+    for b in range(4):
+        op("g", lambda e: e.affine_select(T.eb[:, 512 * b:512 * b + 512], T.one[:], [[1, 512]], A.is_equal, 0.0, -b, -4),
+           [("one", 0, 512)], [("eb", 512 * b, 512 * b + 512)])
+
+    def turn(c0):
+        s0 = c0 + 16
+        op("v", lambda e: e.transpose(T.tt[:, 0:C], T.gg[:, s0:s0 + C]), [("gg", s0, s0 + C)], [("tt", 0, C)])
+        op("v", lambda e: e.transpose(T.tt[:, C:672], T.gg[:, c0:c0 + 352]), [("gg", c0, c0 + 352)], [("tt", C, 672)])
+
+    TT = T.tt[:, 0:672]
+
+    def wrapped(nm, a, by, plus):
+        out = T[nm][:, a:a + 32]
+        tts(out, TT.indirect(T.sel[:, 0:2]), by, plus, A.mult, A.add, [("tt", 0, 672), ("sel", 0, 2)], [(nm, a, a + 32)])
+
+    PARTS = [(0, 128), (128, C)]
+
+    def qstate(r, i):
+        a, b = PARTS[i]
+        quant("xq%d" % r, "xs%d" % r, a, b, "xt%d" % r, 4 * a, 4 * b)
+
+    def score(r, i):
+        a, b = PARTS[i]
+        mul(4 + i, b - a, "uq", "us", 0, "xq%d" % r, "xs%d" % r, a, b)
+
+    def sign(i):
+        a, b = PARTS[i]
+        tts(T.bits[:, a:b], T.ps[:, 512 * (4 + i):512 * (4 + i) + b - a], 0.0, col(0), A.is_gt, A.mult, [bank(4 + i)] + cc(0), [("bits", a, b)])
+
+    quant("uq", "us", 0, 128, "ub", 0, 512)
+    for i in range(2):
+        qstate(0, i)
+        score(0, i)
+    for i in range(2):
+        sign(i)
+
+    GA, GB = 0, 352
+
+    def register(r):
+        kof = "kof%d" % r
+        ttt(T.gg[:, 16:16 + HALF], T.bits[:, 0:C].indirect(T[kof][:, 0:10]), T.k1[:], A.add,
+            [("bits", 0, C), (kof, 0, 10), ("k1", 0, HALF)], [("gg", 16, 16 + HALF)])
+        ttt(T.gg[:, 176:336], T.k3[:], T.gg[:, 16:176], A.subtract, [("k3", 0, HALF), ("gg", 16, 176)], [("gg", 176, 336)])
+        turn(GA)
+        wrapped("of0", 0, 1.0, 160.0)
+        for t in range(4):
+            if t == 3:
+                for o, nm, hi, by in ((T.dat[:, 2:64:4], "dat", 64, 1.0), (T.sd[:], "sd", 16, -2.0)):
+                    op("a", lambda e: e.activation(o, TT.indirect(T.sel[:, 0:1]), ACT.Copy, scale=by),
+                       [("tt", 0, 672), ("sel", 0, 1)], [(nm, 0, hi)])
+            op("a", lambda e: e.activation(T["yp%d" % r][:, C * t:C * t + C],
+                                           T["xt%d" % r][:, 0:4 * C].indirect(T["k4%d" % r][:, 32 * t:32 * t + 20]), ACT.Copy, scale=0.5),
+               [("xt%d" % r, 0, 4 * C), ("k4%d" % r, 32 * t, 32 * t + 20)], [("yp%d" % r, C * t, C * t + C)])
+        cur, nxt, base = GA, GB, "bs0"
+        for i, rad in enumerate(RADIX):
+            of = "of%d" % (i % 2)
+            if i == 2:
+                ttt(T.dl[:, 2:64:4], T.sd[:], T.dat[:, 3:64:4], A.add, [("sd", 0, 16), ("dat", 0, 64)], [("dl", 0, 64)])
+            for j in range(rad - 1):
+                ttt(T.gg[:, nxt + 16:nxt + 336], T.gg[:, cur + 16:cur + 336].indirect(T[of][:, 0:20]), T[base][:], A.min,
+                    [("gg", cur + 16, cur + 336), (of, 0, 20), (base, 0, C)], [("gg", nxt + 16, nxt + 336)])
+                cur, nxt = nxt, cur
+            turn(cur)
+            if i + 1 < len(RADIX):
+                base = "bs%d" % (1 + i % 2)
+                op("a", lambda e: e.activation(T[base][:], T.gg[:, cur + 16:cur + 336], ACT.Identity, bias=col(1)),
+                   [("gg", cur + 16, cur + 336)] + cc(1), [(base, 0, C)])
+                op("a", lambda e: e.activation(T["yi%d" % r][:, C * i:C * i + C], T["yp%d" % r][:, C * i:C * i + C], ACT.Copy),
+                   [("yp%d" % r, C * i, C * i + C)], [("yi%d" % r, C * i, C * i + C)])
+                wrapped("of%d" % ((i + 1) % 2), 0, 1.0, 160.0)
+        for c, ct, sl in ((4, "ct1", 0), (2, "ct0", 1)):
+            ttt(T.dat[:, sl:64:4], TT.indirect(T.sel[:, c:c + 1]), T[ct][:], A.is_equal,
+                [("tt", 0, 672), ("sel", c, c + 1), (ct, 0, 16)], [("dat", 0, 64)])
+        op("v", lambda e: e.tensor_tensor_scan(T.sc[:], T.dl[:], T.dat[:], 0.0, A.mult, A.add), [("dl", 0, 64), ("dat", 0, 64)], [("sc", 0, 64)])
+        tof = "tof%d" % r
+        for h in range(2):
+            tts(T[tof][:, 10 * h:10 * h + 10], T.sc[:, 2 + h:39 + h:4], 160.0, None, A.add, None, [("sc", 0, 64)], [(tof, 10 * h, 10 * h + 10)])
+
+    def pairs(r, a, b):
+        for t in range(4):
+            yp, yi, tof = "yp%d" % r, "yi%d" % r, "tof%d" % r
+            ttt(T["zt%d" % r][:, 4 * a + t:4 * b:4], T[yp][:, C * t:C * t + C].indirect(T[tof][:, a // 16:b // 16]),
+                T[yi][:, C * t + a:C * t + b], A.add, [(yp, C * t, C * t + C), (yi, C * t + a, C * t + b), (tof, a // 16, b // 16)], [("zt%d" % r, 4 * a, 4 * b)])
+
+    def layer(r, zcol, bk):
+        for b in range(4):
+            mul(bk + b, 128, "wq", "wp", 128 * b, "zq%d" % r, "zs%d" % r, zcol, zcol + 128)
+
+    def keep(r, a, bk):
+        for b in range(4):
+            op("a", lambda e: e.activation(T["ht%d" % r][:, 4 * a + b:4 * a + 512:4], T.ps[:, 512 * (bk + b):512 * (bk + b) + 128], ACT.Copy, scale=0.03125),
+               [bank(bk + b)], [("ht%d" % r, 4 * a, 4 * a + 512)])
+
+    def ship(r, i):
+        a = 128 * i
+        quant("hq%d" % r, "hs%d" % r, a, a + 128, "ht%d" % r, 4 * a, 4 * a + 512)
+        sem = "ar%d%d" % (i, r)
+        send(peer[r], T["rq%d" % r][:, a:a + 128].bitcast(dt.uint8), T["hq%d" % r][:, a:a + 128].bitcast(dt.uint8), [("hq%d" % r, a, a + 128)], sem)
+        send(peer[r], T["rs%d" % r][:, a:a + 128], T["hs%d" % r][:, a:a + 128], [("hs%d" % r, a, a + 128)], sem)
+
+    def unpack(r, i, bk):
+        a = 128 * i
+        sem = "ar%d%d" % (i, r)
+        note("net", [], [("rq%d" % r, a, a + 128), ("rs%d" % r, a, a + 128)], sem, total[sem])
+        for b in range(4):
+            mul(bk + b, 128, "eq", "ep", 128 * b, "rq%d" % r, "rs%d" % r, a, a + 128)
+        for b in range(4):
+            o, p = T["bp%d" % r][:, C * b + a:C * b + a + 128], T.ps[:, 512 * (bk + b):512 * (bk + b) + 128]
+            w = [("bp%d" % r, C * b + a, C * b + a + 128)]
+            if b % 2 == 0:
+                op("v", lambda e: e.tensor_copy(o, p), [bank(bk + b)], w)
+            else:
+                op("a", lambda e: e.activation(o, p, ACT.Copy), [bank(bk + b)], w)
+
+    def advance(r, i):
+        a, b = PARTS[i]
+        for t in range(4):
+            bp, kof = "bp%d" % r, "kof%d" % (r + 1)
+            ttt(T["xt%d" % (r + 1)][:, 4 * a + t:4 * b:4], T[bp][:, C * t:C * t + C].indirect(T[kof][:, a // 16:b // 16]),
+                T["xt%d" % r][:, 4 * a + t:4 * b:4], A.add,
+                [(bp, C * t, C * t + C), (kof, a // 16, b // 16), ("xt%d" % r, 4 * a, 4 * b)], [("xt%d" % (r + 1), 4 * a, 4 * b)])
+
+    for r in range(ROUNDS):
+        register(r)
+        nr = 352 * (2 + r)
+        kr, kk, kof, tof = C * r, "kk%d" % r, "kof%d" % r, "tof%d" % r
+        op("a", lambda e: e.activation(T[kk][:], T.krs[:, kr:kr + C].indirect(T[kof][:, 0:20]), ACT.Copy),
+           [("krs", kr, kr + C), (kof, 0, 20)], [(kk, 0, C)])
+        op("a", lambda e: e.activation(T.gg[:, nr + 16:nr + 336], T[kk][:, 0:C].indirect(T[tof][:, 0:20]), ACT.Copy),
+           [(kk, 0, C), (tof, 0, 20)], [("gg", nr + 16, nr + 336)])
+        zq, zs, zt = "zq%d" % r, "zs%d" % r, "zt%d" % r
+        for i in range(2):
+            pairs(r, 128 * i, 128 * i + 128)
+            quant(zq, zs, 128 * i, 128 * i + 128, zt, 512 * i, 512 * i + 512)
+            layer(r, 128 * i, 4 * i)
+            keep(r, 128 * i, 4 * i)
+        ship(r, 0)
+        pairs(r, CROSS, C)
+        quant(zq, zs, 256, 384, zt, 4 * 192, 4 * C)
+        layer(r, 256, 0)
+        for b in range(4):
+            op("a", lambda e: e.activation(T["bp%d" % r][:, C * b + CROSS:C * b + C], T.ps[:, 512 * b + 64:512 * b + 128], ACT.Copy, scale=0.03125),
+               [bank(b)], [("bp%d" % r, C * b + CROSS, C * b + C)])
+        ship(r, 1)
+        turn(nr)
+        wrapped("kof%d" % (r + 1), 0, 1.0, 160.0)
+        if r + 1 < ROUNDS:
+            k4 = "k4%d" % (r + 1)
+            for t in range(4):
+                wrapped(k4, 32 * t, 4.0, 640.0 + t)
+            dma("s", "dk%d" % (r + 1), [(T["lk%d" % (r + 1)][:, :], T.gg[0:128:16, nr + 16:nr + 336],
+                                         [("gg", nr + 16, nr + 336)], [("lk%d" % (r + 1), 0, 160)])])
+            share(r + 1)
+        else:
+            tts(T.kpf[:], T.gg[:, nr + 16:nr + 336], 160.0, None, A.add, None, [("gg", nr + 16, nr + 336)], [("kpf", 0, C)])
+            dma("s", "okp", [(T.kp[:, :], T.kpf[0:128:16, :], [("kpf", 0, C)], [])])
+            quant("vq", "vs", 0, 128, "vb", 0, 512)
+        if r == 0:
+            quant("eq", "ep", 0, 512, "eb", 0, 2048)
+        unpack(r, 0, 4)
+        unpack(r, 1, 0)
+        n = r + 1
+        if n < ROUNDS:
+            advance(r, 0)
+            qstate(n, 0)
+            score(n, 0)
+            advance(r, 1)
+            sign(0)
+            qstate(n, 1)
+            score(n, 1)
+            sign(1)
+        else:
+            for i in range(2):
+                a, b = PARTS[i]
+                advance(r, i)
+                qstate(n, i)
+                mul(4 + i, b - a, "vq", "vs", 0, "xq%d" % n, "xs%d" % n, a, b)
+                op("a", lambda e: e.activation(T.yo[:, a:b], T.ps[:, 512 * (4 + i):512 * (4 + i) + b - a], ACT.Copy), [bank(4 + i)], [("yo", a, b)])
+                dma("s", "oc%d" % i, [(T.oc[:, 4 * a:4 * b], T["xq%d" % n][:, a:b].bitcast(dt.uint8), [("xq%d" % n, a, b)], [])])
+                dma("a", "oy%d" % i, [(T.y[:, a:b], T.yo[:, a:b], [("yo", a, b)], [])])
+            dma("s", "os", [(T.osc[4 * i:4 * i + 4, :], T["xs%d" % n][32 * i:32 * i + 4, :], [("xs%d" % n, 0, C)], []) for i in range(4)])
+    for sem in total:
+        if seen["g"].get(sem, 0) < total[sem]:
+            g.wait_ge(T.sem[sem], total[sem])

@@ -3,8 +3,15 @@ from concourse.mybir import dt, AluOpType, ActivationFunctionType
 C, HALF, CROSS = 320, 160, 256
 ROUNDS = 3
 MASKS = [1, 2, 3]
-RADIX = [3, 3, 3, 3, 4]
-BIG = 1024.0
+LONG = [(0, 2), (4, 8), (11, 12), (14, 20)]
+SHORT = [(2, 4), (8, 11), (12, 14)]
+BLOCKS = [b for a, e in LONG + SHORT for b in range(a, e)]
+AT = {b: i for i, b in enumerate(BLOCKS)}
+NB = sum(e - a for a, e in LONG)
+NL, NS = 16 * NB, C - 16 * NB
+RADIX = [3, 3, 3, 3, 3]
+BIG, LESS = 1024.0, 256
+G0 = NL + 16
 F32, BF, I32, U16, F8, U8 = "float32", "bfloat16", "int32", "uint16", "float8_e4m3fn_x4", "uint8"
 
 SCRATCH = {
@@ -14,16 +21,19 @@ SCRATCH = {
     "wq": ("sbuf", [128, 512], F8), "wp": ("sbuf", [128, 512], U8),
     "one": ("sbuf", [128, 512], BF), "eb": ("sbuf", [128, 2048], BF),
     "eq": ("sbuf", [128, 512], F8), "ep": ("sbuf", [128, 512], U8),
-    "pidx": ("sbuf", [128, 1], I32), "qidx": ("sbuf", [128, 1], I32), "grp": ("sbuf", [128, 1], I32), "par": ("sbuf", [128, 1], I32),
-    "yrow": ("sbuf", [128, C], F32), "cwi": ("sbuf", [128, 16], F32), "cst": ("sbuf", [128, 16], F32), "sel": ("sbuf", [128, 8], U16),
-    "k1": ("sbuf", [128, HALF], BF), "k3": ("sbuf", [128, HALF], F32), "bs0": ("sbuf", [128, C], BF),
+    "pidx": ("sbuf", [128, 1], I32), "qidx": ("sbuf", [128, 1], I32), "grp": ("sbuf", [128, 1], I32),
+    "yrow": ("sbuf", [128, C], F32), "cwi": ("sbuf", [128, 16], F32), "cst": ("sbuf", [128, 16], F32), "sel": ("sbuf", [128, 12], U16),
+    "rt": ("sbuf", [128, 128], F32), "ru": ("sbuf", [128, 128], F32), "ki": ("sbuf", [128, 5], I32), "kf": ("sbuf", [128, 5], F32),
+    "dr": ("sbuf", [128, HALF], F32), "d1": ("sbuf", [128, HALF], F32), "k1b": ("sbuf", [128, HALF], F32), "k3b": ("sbuf", [128, HALF], F32),
+    "k1": ("sbuf", [128, HALF], BF), "k3": ("sbuf", [128, HALF], F32), "bs0": ("sbuf", [128, NL], BF),
     "cw": ("sbuf", [128, 16], F32), "ca": ("sbuf", [128, 16], F32), "cb": ("sbuf", [128, 16], F32), "cd": ("sbuf", [128, 16], F32),
-    "ct0": ("sbuf", [128, 16], F32), "ct1": ("sbuf", [128, 16], F32),
-    "dl": ("sbuf", [128, 64], F32), "dat": ("sbuf", [128, 64], F32), "sc": ("sbuf", [128, 64], F32), "sd": ("sbuf", [128, 16], F32),
+    "c2": ("sbuf", [128, 16], F32), "ct0": ("sbuf", [128, 16], F32), "ct1": ("sbuf", [128, 16], F32),
+    "dl": ("sbuf", [128, 64], F32), "dat": ("sbuf", [128, 64], F32), "sc": ("sbuf", [128, 64], F32),
+    "fi": ("sbuf", [128, 16], I32), "fa": ("sbuf", [128, 16], I32),
     "kli": ("sbuf", [128, 20], I32), "klb": ("sbuf", [128, 32], BF), "klt": ("sbuf", [128, 32], BF),
-    "gg": ("sbuf", [128, 5 * 352], BF), "krs": ("sbuf", [128, 3 * C], BF),
-    "bits": ("sbuf", [128, C], BF), "bs1": ("sbuf", [128, C], BF), "bs2": ("sbuf", [128, C], BF),
-    "tt": ("sbuf", [128, 672], BF), "of0": ("sbuf", [128, 32], U16), "of1": ("sbuf", [128, 32], U16),
+    "w0": ("sbuf", [128, G0 + C + 16], BF), "gg": ("sbuf", [128, 5 * 352], BF), "krs": ("sbuf", [128, 3 * C], BF),
+    "bits": ("sbuf", [128, C], BF), "bs1": ("sbuf", [128, NL], BF), "bs2": ("sbuf", [128, NL], BF),
+    "tt": ("sbuf", [128, 864], BF), "of0": ("sbuf", [128, 16], U16), "of1": ("sbuf", [128, 16], U16), "ofs": ("sbuf", [128, 16], U16),
     "kpf": ("sbuf", [128, C], F32), "yo": ("sbuf", [128, C], F32),
     "ps": ("psum", [128, 4096], F32),
 }
@@ -120,6 +130,9 @@ def rank_program(g, core, T, topo):
     def ttt(out, in0, in1, o, reads, writes):
         op("v", lambda e: e.tensor_tensor(out, in0, in1, o), reads, writes)
 
+    def act(out, in_, f, reads, writes, **k):
+        op("a", lambda e: e.activation(out, in_, f, **k), reads, writes)
+
     def quant(q, s, a, b, t, ta, tb):
         op("v", lambda e: e.quantize_mx(T[q][:, a:b], T[s][:, a:b], T[t][:, ta:tb]), [(t, ta, tb)], [(q, a, b), (s, a, b)])
 
@@ -132,21 +145,20 @@ def rank_program(g, core, T, topo):
            [(lq, l, l + 128), (ls, l, l + 128), (rq, a, b), (rs, a, b)], [bank(i)])
 
     peer = [T.cores[rank ^ m] for m in MASKS]
-    dma("s", "lx0", [(T.xt0[:, 0:512], T.x[:, 0:512], [], [("xt0", 0, 512)])])
+    dma("s", "lx0", [(T.xt0[:, 0:768], T.x[:, 0:768], [], [("xt0", 0, 768)])])
     dma("a", "lk", [(T.kli[:], T.kl[:, :], [], [("kli", 0, 20)])])
-    dma("s", "lx1", [(T.xt0[:, 512:1280], T.x[:, 512:1280], [], [("xt0", 512, 1280)])])
+    dma("s", "lx1", [(T.xt0[:, 768:1280], T.x[:, 768:1280], [], [("xt0", 768, 1280)])])
     dma("a", "lu", [(T.ub[:], T.u[:, :], [], [("ub", 0, 512)])])
     dma("s", "lwc", [(T.wq[:, 0:512].bitcast(dt.uint8), T.wc[:, 0:2048], [], [("wq", 0, 512)])])
     dma("s", "lws", [(T.wp[:, 0:512], T.ws[:, 0:512], [], [("wp", 0, 512)])])
     dma("a", "lv", [(T.vb[:], T.v[:, :], [], [("vb", 0, 512)])])
 
-    op("g", lambda e: e.iota(T.pidx[:], [[0, 1]], 0, 1), [], [("pidx", 0, 1)])
-    op("g", lambda e: e.iota(T.yrow[:], [[1, C]], 0, 0, allow_small_or_imprecise_dtypes=True), [], [("yrow", 0, C)])
-    op("g", lambda e: e.iota(T.cwi[:], [[16, 16]], 0, 1, allow_small_or_imprecise_dtypes=True), [], [("cwi", 0, 16)])
-    op("v", lambda e: e.memset(T.klb[:], 0.0), [], [("klb", 0, 32)])
-    op("v", lambda e: e.memset(T.one[:], 1.0), [], [("one", 0, 512)])
-    op("v", lambda e: e.memset(T.dl[:, 0:64:4], 0.0), [], [("dl", 0, 64)])
-    op("v", lambda e: e.memset(T.dl[:, 3:64:4], -1.0), [], [("dl", 0, 64)])
+    later = []
+
+    def drip(n):
+        for call in later[:n]:
+            call()
+        later[:n] = []
 
     def col(i):
         return T.cst[:, i:i + 1]
@@ -156,65 +168,129 @@ def rank_program(g, core, T, topo):
 
     def scol(i, in0, names, s1, s2, o0, o1):
         tts(col(i), in0, s1, s2, o0, o1, names, cc(i))
-    P1, Q1, G1, PA = ("pidx", 0, 1), ("qidx", 0, 1), ("grp", 0, 1), ("par", 0, 1)
+    P1, Q1, GR, YR = ("pidx", 0, 1), ("qidx", 0, 1), ("grp", 0, 1), ("yrow", 0, C)
+    op("g", lambda e: e.iota(T.pidx[:], [[0, 1]], 0, 1), [], [P1])
+    op("g", lambda e: e.iota(T.yrow[:], [[1, C]], 0, 0, allow_small_or_imprecise_dtypes=True), [], [YR])
+    op("g", lambda e: e.iota(T.cwi[:], [[16, 16]], 0, 1, allow_small_or_imprecise_dtypes=True), [], [("cwi", 0, 16)])
+    op("v", lambda e: e.memset(T.rt[:], 0.0), [], [("rt", 0, 128)])
+    op("v", lambda e: e.memset(T.one[:], 1.0), [], [("one", 0, 512)])
+    op("v", lambda e: e.memset(T.klb[:], 0.0), [], [("klb", 0, 32)])
+    cuts = sorted([(a, e, 16 * (AT[a] - a)) for a, e in LONG] + [(a, e, G0) for a, e in SHORT])
+    for a, e, d in cuts:
+        op("v", lambda x: x.memset(T.dr[:, 8 * a:8 * e], float(d)), [], [("dr", 8 * a, 8 * e)])
     tts(T.qidx[:], T.pidx[:], 15, None, A.bitwise_and, None, [P1], [Q1])
-    tts(T.grp[:], T.pidx[:], 4, None, A.arith_shift_right, None, [P1], [G1])
+    tts(T.grp[:], T.pidx[:], 4, None, A.arith_shift_right, None, [P1], [GR])
     scol(0, T.qidx[:], [Q1], 0.0, None, A.is_equal, None)
     scol(1, T.qidx[:], [Q1], 0.0, BIG, A.is_equal, A.mult)
-    ttt(T.par[:], T.pidx[:], T.grp[:], A.add, [P1, G1], [PA])
-    scol(12, T.qidx[:], [Q1], 16.0, None, A.mult, None)
-    scol(8, T.grp[:], [G1], 16.0, None, A.mult, None)
-    scol(5, col(0), cc(0), 2.0, 2.0, A.mult, A.add)
-    scol(6, col(0), cc(0), -479.0, 160.0, A.mult, A.add)
-    tts(T.par[:], T.par[:], 1, None, A.bitwise_and, None, [PA], [PA])
-    scol(7, col(0), cc(0), -160.0, None, A.mult, None)
-    scol(4, col(0), cc(0), 1.0, None, A.add, None)
-    scol(10, T.qidx[:], [Q1], 4.0, 256.0, A.is_lt, A.mult)
-    scol(11, T.qidx[:], [Q1], 10.0, 160.0, A.is_lt, A.mult)
-    scol(9, T.par[:], [PA] + cc(12), 336.0, col(12), A.mult, A.add)
-    tts(T.cw[:], T.cwi[:], col(8), None, A.subtract, None, [("cwi", 0, 16)] + cc(8), [("cw", 0, 16)])
+    scol(8, T.grp[:], [GR], 1.0, None, A.mult, None)
+    scol(9, T.grp[:], [GR], 16.0, None, A.mult, None)
+    scol(2, col(0), cc(0), 1.0, None, A.add, None)
+    scol(3, col(0), cc(0), float(-LESS), None, A.mult, None)
+    scol(4, col(0), cc(0), 2.0, 2.0, A.mult, A.add)
+    scol(5, col(0), cc(0), float(1 - 2 * LESS - HALF), float(HALF), A.mult, A.add)
+    scol(6, col(0), cc(0), -LESS - BIG, BIG, A.mult, A.add)
 
-    def widen(nm, n, scale, bias, names):
-        op("a", lambda e: e.activation(T[nm][:, 0:n], T.yrow[:, 0:n], ACT.Identity, bias=bias, scale=scale),
-           [("yrow", 0, C)] + names, [(nm, 0, n)])
-    widen("k1", HALF, col(4), col(7), cc(4, 7))
-    widen("k3", HALF, col(5), col(6), cc(5, 6))
-    widen("bs0", C, 1.0, col(1), cc(1))
+    def widen(nm, a, b, src, c, scale, bias, names):
+        act(T[nm][:, a:b], T[src][:, c:c + b - a], ACT.Identity, [(src, c, c + b - a)] + names, [(nm, a, b)], bias=bias, scale=scale)
 
     def blank(nm, a, b):
-        op("a", lambda e: e.activation(T[nm][:, a:b], T.yrow[:, 0:b - a], ACT.Copy, scale=0.0), [("yrow", 0, C)], [(nm, a, b)])
-    for a, b in ((0, 16), (336, 368), (688, 720), (1040, 1072), (1392, 1424), (1744, 1760)):
-        blank("gg", a, b)
-    for i in range(ROUNDS):
-        blank("krs", C * i, C * i + C)
-    for c, i, row in ((0, None, 0), (1, 10, 0), (2, None, 1), (4, 11, 1)):
-        if i is None:
-            tts(T.sel[:, c:c + 1], col(9), float(row), None, A.add, None, cc(9), [("sel", c, c + 1)])
-        else:
-            tts(T.sel[:, c:c + 1], col(9), float(row), col(i), A.add, A.add, cc(9, i), [("sel", c, c + 1)])
-    CW = [("cw", 0, 16)]
-    tts(T.ca[:], T.cw[:], 0.0, None, A.is_equal, None, CW, [("ca", 0, 16)])
-    tts(T.cb[:], T.cw[:], 159.0, -160.0, A.is_equal, A.mult, CW, [("cb", 0, 16)])
-    tts(T.cd[:], T.cw[:], 159.0, 161.0, A.is_equal, A.mult, CW, [("cd", 0, 16)])
-    tts(T.dl[:, 1:64:4], T.cw[:], 159.0, 2.0, A.is_equal, A.mult, CW, [("dl", 0, 64)])
-    tts(T.dat[:, 3:64:4], T.cw[:], 4.0, -319.0, A.mult, A.add, CW, [("dat", 0, 64)])
-    ttt(T.ca[:], T.cw[:], T.ca[:], A.subtract, CW + [("ca", 0, 16)], [("ca", 0, 16)])
-    tts(T.dl[:, 1:64:4], T.dl[:, 1:64:4], -1.0, None, A.add, None, [("dl", 0, 64)], [("dl", 0, 64)])
-    ttt(T.ct0[:], T.ca[:], T.cb[:], A.add, [("ca", 0, 16), ("cb", 0, 16)], [("ct0", 0, 16)])
-    ttt(T.ct1[:], T.ca[:], T.cd[:], A.add, [("ca", 0, 16), ("cd", 0, 16)], [("ct1", 0, 16)])
+        act(T[nm][:, a:b], T.yrow[:, 0:b - a], ACT.Copy, [YR], [(nm, a, b)], scale=0.0)
+    lists = [LONG, SHORT]
+    for h in (0, 10):
+        runs = []
+        for b in range(h, h + 10):
+            if runs and AT[b] == runs[-1][1]:
+                runs[-1][1] += 1
+            else:
+                runs.append([AT[b], AT[b] + 1])
+        lists.append(runs)
 
+    def row_of(i):
+        for j in (32 * i, 32 * i + 16):
+            for a, e in lists[i]:
+                w = ("rt", j, j + e - a)
+                if i < 2:
+                    act(T.rt[:, j:j + e - a], T.yrow[:, a:e], ACT.Copy, [YR, w], [w])
+                else:
+                    op("g", lambda x: x.iota(T.rt[:, j:j + e - a], [[1, e - a]], a, 0, allow_small_or_imprecise_dtypes=True), [w], [w])
+                j += e - a
+    row_of(2)
+    row_of(3)
+    widen("k1b", 0, HALF, "yrow", 0, col(2), col(3), cc(2, 3))
+    widen("d1", 0, HALF, "dr", 0, col(0), 0.0, cc(0))
+    widen("k3b", 0, HALF, "yrow", 0, col(4), col(5), cc(4, 5))
+    row_of(0)
+    row_of(1)
+    blank("tt", 672, 864)
+    ttt(T.k1[:], T.k1b[:], T.d1[:], A.add, [("k1b", 0, HALF), ("d1", 0, HALF)], [("k1", 0, HALF)])
+    tts(T.d1[:], T.d1[:], 2.0, None, A.mult, None, [("d1", 0, HALF)], [("d1", 0, HALF)])
     KL = [("kli", 0, 20)]
     tts(T.klb[:, 0:20], T.kli[:], -160.0, None, A.add, None, KL, [("klb", 0, 20)])
     tts(T.kof0[:, 0:20], T.kli[:], 0.0, None, A.add, None, KL, [("kof0", 0, 20)])
+    ttt(T.k3[:], T.k3b[:], T.d1[:], A.add, [("k3b", 0, HALF), ("d1", 0, HALF)], [("k3", 0, HALF)])
     op("v", lambda e: e.transpose(T.klt[:], T.klb[:]), [("klb", 0, 32)], [("klt", 0, 32)])
-    for t in range(4):
-        tts(T.k40[:, 32 * t:32 * t + 20], T.kli[:], 4.0, float(t), A.mult, A.add, KL, [("k40", 32 * t, 32 * t + 20)])
+    WIDE = 32 * ((NB + 1) // 2)
+    RU, KI, KF = [("ru", 0, 128)], [("ki", 0, 4)], [("kf", 0, 4)]
+    KQ = [("ki", 4, 5), ("kf", 4, 5)]
+
+    def seln(o, in0, s1, s2, o0, o1, names):
+        tts(o, in0, s1, s2, o0, o1, names, [("sel", 0, 12)])
+    tts(T.ki[:, 4:5], T.qidx[:], col(8), None, A.add, None, [Q1] + cc(8), [("ki", 4, 5)])
+    tts(T.kf[:, 4:5], T.qidx[:], 16.0, None, A.mult, None, [Q1], [("kf", 4, 5)])
+
+    def own_places():
+        tts(T.ki[:, 4:5], T.ki[:, 4:5], 1, None, A.bitwise_and, None, [("ki", 4, 5)], [("ki", 4, 5)])
+        for t in range(4):
+            tts(T.k40[:, 32 * t:32 * t + 20], T.kli[:], 4.0, float(t), A.mult, A.add, KL, [("k40", 32 * t, 32 * t + 20)])
+        seln(T.sel[:, 6:7], T.ki[:, 4:5], float(WIDE + 16), T.kf[:, 4:5], A.mult, A.add, KQ)
+        seln(T.sel[:, 0:1], T.ki[:, 4:5], float(C + 16), T.kf[:, 4:5], A.mult, A.add, KQ)
+
+    where = [
+        lambda: op("v", lambda e: e.transpose(T.ru[:], T.rt[:]), [("rt", 0, 128)], RU),
+        lambda: (tts(T.ki[:, 0:4], T.ru[:, 0:128:32], col(8), None, A.add, None, RU + cc(8), KI),
+                 tts(T.kf[:, 0:4], T.ru[:, 0:128:32], 16.0, None, A.mult, None, RU, KF)),
+        lambda: tts(T.ki[:, 0:4], T.ki[:, 0:4], 1, None, A.bitwise_and, None, KI, KI),
+        lambda: tts(T.ki[:, 0:4], T.ki[:, 0:4], C + 16, None, A.mult, None, KI, KI),
+        lambda: ttt(T.kf[:, 0:4], T.kf[:, 0:4], T.ki[:, 0:4], A.add, KI + KF, KF),
+        lambda: seln(T.sel[:, 2:6:2], T.kf[:, 0:2], 0.0, None, A.add, None, KF)]
+
+    def find(i):
+        where[i]()
+    later += [lambda: seln(T.sel[:, 8:12:2], T.kf[:, 2:4], 1.0, None, A.add, None, KF),
+              lambda: seln(T.sel[:, 1:2], T.sel[:, 0:1], 256.0, None, A.add, None, [("sel", 0, 12)])]
+    SE = ("sel", 0, 12)
+    for a, e in LONG:
+        widen("bs0", 16 * AT[a], 16 * (AT[a] + e - a), "yrow", 16 * a, 1.0, col(1), cc(1))
+    widen("w0", 0, NL, "yrow", 0, col(0), col(6), cc(0, 6))
+    blank("w0", NL, G0)
+    blank("w0", G0 + C, G0 + C + 16)
+    for i in range(2):
+        blank("gg", 352 * i, 352 * i + 16)
+        blank("gg", 352 * i + 16 + NL, 352 * i + 352)
+    CW = [("cw", 0, 16)]
+    later += [
+        lambda: tts(T.cw[:], T.cwi[:], col(9), None, A.subtract, None, [("cwi", 0, 16)] + cc(9), CW),
+        lambda: op("v", lambda e: e.memset(T.dl[:, 0:64:4], 0.0), [], [("dl", 0, 64)]),
+        lambda: tts(T.c2[:], T.cw[:], 2.0, -160.0, A.mult, A.add, CW, [("c2", 0, 16)]),
+        lambda: op("v", lambda e: e.memset(T.dl[:, 3:64:4], -1.0), [], [("dl", 0, 64)]),
+        lambda: tts(T.dat[:, 3:64:4], T.cw[:], 4.0, -319.0, A.mult, A.add, CW, [("dat", 0, 64)]),
+        lambda: tts(T.ca[:], T.cw[:], 0.0, None, A.is_equal, None, CW, [("ca", 0, 16)]),
+        lambda: tts(T.dl[:, 1:64:4], T.cw[:], 159.0, 2.0, A.is_equal, A.mult, CW, [("dl", 0, 64)]),
+        lambda: tts(T.cb[:], T.cw[:], 159.0, -160.0, A.is_equal, A.mult, CW, [("cb", 0, 16)]),
+        lambda: ttt(T.ca[:], T.cw[:], T.ca[:], A.subtract, CW + [("ca", 0, 16)], [("ca", 0, 16)]),
+        lambda: tts(T.dl[:, 1:64:4], T.dl[:, 1:64:4], -1.0, None, A.add, None, [("dl", 0, 64)], [("dl", 0, 64)]),
+        lambda: tts(T.cd[:], T.cw[:], 159.0, 161.0, A.is_equal, A.mult, CW, [("cd", 0, 16)]),
+        lambda: ttt(T.ct0[:], T.ca[:], T.cb[:], A.add, [("ca", 0, 16), ("cb", 0, 16)], [("ct0", 0, 16)]),
+        lambda: ttt(T.ct1[:], T.ca[:], T.cd[:], A.add, [("ca", 0, 16), ("cd", 0, 16)], [("ct1", 0, 16)])]
+
     dma("s", "dk0", [(T.lk0[16 * i:16 * i + 16, :], T.klt[32 * (i // 2):32 * (i // 2) + 20, 16 * (i % 2):16 * (i % 2) + 16],
                       [("klt", 0, 32)], [("lk0", 20 * i, 20 * i + 20)]) for i in range(8)])
 
     def share(r):
         send(peer[r], T["rk%d" % r][:, :], T["lk%d" % r][:, :], [("lk%d" % r, 0, 160)], "arl%d" % r)
         note("net", [], [("rk%d" % r, 0, 160)], "arl%d" % r, total["arl%d" % r])
+
+    def fetch(r):
         dma("s", "dr%d" % r, [(T.krs[0:128:16, C * r:C * r + C], T["rk%d" % r][:, :],
                                [("rk%d" % r, 0, 160)], [("krs", C * r, C * r + C)])])
 
@@ -223,18 +299,26 @@ def rank_program(g, core, T, topo):
         op("g", lambda e: e.affine_select(T.eb[:, 512 * b:512 * b + 512], T.one[:], [[1, 512]], A.is_equal, 0.0, -b, -4),
            [("one", 0, 512)], [("eb", 512 * b, 512 * b + 512)])
 
-    def turn(c0):
-        s0 = c0 + 16
-        op("v", lambda e: e.transpose(T.tt[:, 0:C], T.gg[:, s0:s0 + C]), [("gg", s0, s0 + C)], [("tt", 0, C)])
-        op("v", lambda e: e.transpose(T.tt[:, C:672], T.gg[:, c0:c0 + 352]), [("gg", c0, c0 + 352)], [("tt", C, 672)])
+    def flip(to, nm, c, n):
+        op("v", lambda e: e.transpose(T.tt[:, to:to + n], T[nm][:, c:c + n]), [(nm, c, c + n)], [("tt", to, to + n)])
 
-    TT = T.tt[:, 0:672]
+    def turn(nm, c0, cut, ahead=None, between=None):
+        if ahead is not None:
+            ahead()
+        flip(0, nm, c0 + 16, cut)
+        flip(C, nm, c0, cut)
+        if between is not None:
+            between()
+        flip(cut, nm, c0 + 16 + cut, C - cut)
+        flip(C + cut, nm, c0 + cut, C + 32 - cut)
 
-    def wrapped(nm, a, by, plus):
-        out = T[nm][:, a:a + 32]
-        tts(out, TT.indirect(T.sel[:, 0:2]), by, plus, A.mult, A.add, [("tt", 0, 672), ("sel", 0, 2)], [(nm, a, a + 32)])
+    TT, TN = T.tt[:, 0:864], ("tt", 0, 864)
 
-    PARTS = [(0, 128), (128, C)]
+    def wrapped(nm, a, wide, sel, by, plus):
+        tts(T[nm][:, a:a + 16 * wide], TT.indirect(T.sel[:, sel:sel + wide]), by, plus, A.mult, A.add,
+            [TN, SE], [(nm, a, a + 16 * wide)])
+
+    PARTS = [(0, 192), (192, C)]
 
     def qstate(r, i):
         a, b = PARTS[i]
@@ -252,53 +336,78 @@ def rank_program(g, core, T, topo):
     for i in range(2):
         qstate(0, i)
         score(0, i)
+    own_places()
     for i in range(2):
+        find(i)
         sign(i)
-
-    GA, GB = 0, 352
 
     def register(r):
         kof = "kof%d" % r
-        ttt(T.gg[:, 16:16 + HALF], T.bits[:, 0:C].indirect(T[kof][:, 0:10]), T.k1[:], A.add,
-            [("bits", 0, C), (kof, 0, 10), ("k1", 0, HALF)], [("gg", 16, 16 + HALF)])
-        ttt(T.gg[:, 176:336], T.k3[:], T.gg[:, 16:176], A.subtract, [("k3", 0, HALF), ("gg", 16, 176)], [("gg", 176, 336)])
-        turn(GA)
-        wrapped("of0", 0, 1.0, 160.0)
-        for t in range(4):
-            if t == 3:
-                for o, nm, hi, by in ((T.dat[:, 2:64:4], "dat", 64, 1.0), (T.sd[:], "sd", 16, -2.0)):
-                    op("a", lambda e: e.activation(o, TT.indirect(T.sel[:, 0:1]), ACT.Copy, scale=by),
-                       [("tt", 0, 672), ("sel", 0, 1)], [(nm, 0, hi)])
-            op("a", lambda e: e.activation(T["yp%d" % r][:, C * t:C * t + C],
-                                           T["xt%d" % r][:, 0:4 * C].indirect(T["k4%d" % r][:, 32 * t:32 * t + 20]), ACT.Copy, scale=0.5),
-               [("xt%d" % r, 0, 4 * C), ("k4%d" % r, 32 * t, 32 * t + 20)], [("yp%d" % r, C * t, C * t + C)])
-        cur, nxt, base = GA, GB, "bs0"
+        H1 = G0 + HALF
+        ttt(T.w0[:, G0:H1], T.bits[:, 0:C].indirect(T[kof][:, 0:10]), T.k1[:], A.add,
+            [("bits", 0, C), (kof, 0, 10), ("k1", 0, HALF)], [("w0", G0, H1)])
+
+        def half(t):
+            act(T["yp%d" % r][:, C * t:C * t + C], T["xt%d" % r][:, 0:4 * C].indirect(T["k4%d" % r][:, 32 * t:32 * t + 20]), ACT.Copy,
+                [("xt%d" % r, 0, 4 * C), ("k4%d" % r, 32 * t, 32 * t + 20)], [("yp%d" % r, C * t, C * t + C)], scale=0.5)
+
+        def again(t):
+            act(T["yi%d" % r][:, C * t:C * t + C], T["yp%d" % r][:, C * t:C * t + C], ACT.Copy,
+                [("yp%d" % r, C * t, C * t + C)], [("yi%d" % r, C * t, C * t + C)])
+
+        def blanks(i):
+            if r == 0:
+                blank("gg", 352 * i + 704, 352 * i + 720)
+                blank("gg", 352 * i + 1040, 352 * i + 1056)
+                blank("krs", C * i, C * i + C)
+        half(0)
+        half(1)
+        aside = [lambda: half(2), lambda: (half(3), again(0)), lambda: (again(1), again(2), blanks(0)),
+                 lambda: (again(3), blanks(1)), lambda: blanks(2)]
+        gap = find if r == 0 else (lambda i: None)
+        gap(2)
+        ttt(T.w0[:, H1:G0 + C], T.k3[:], T.w0[:, G0:H1], A.subtract, [("k3", 0, HALF), ("w0", G0, H1)], [("w0", H1, G0 + C)])
+        gap(3)
+        turn("w0", G0 - 16, HALF, None, lambda: gap(4))
+        gap(5)
+        wrapped("of0", 0, 1, 2, 1.0, float(LESS))
+        wrapped("ofs", 0, 1, 4, 1.0, float(LESS))
+        op("v", lambda e: e.tensor_copy(T.fi[:], TT.indirect(T.sel[:, 0:1])), [TN, SE], [("fi", 0, 16)])
+        cur, nxt = 352, 0
+        ttt(T.gg[:, 16:16 + NL], T.w0[:, 0:G0 + C].indirect(T.of0[:, 0:NB]), T.bs0[:], A.min,
+            [("w0", 0, G0 + C), ("of0", 0, 16), ("bs0", 0, NL)], [("gg", 16, 16 + NL)])
+        cur, nxt = nxt, cur
+        tts(T.fa[:], T.fi[:], 1, None, A.bitwise_and, None, [("fi", 0, 16)], [("fa", 0, 16)])
         for i, rad in enumerate(RADIX):
-            of = "of%d" % (i % 2)
-            if i == 2:
-                ttt(T.dl[:, 2:64:4], T.sd[:], T.dat[:, 3:64:4], A.add, [("sd", 0, 16), ("dat", 0, 64)], [("dl", 0, 64)])
+            base, of = "bs%d" % (1 + i % 2), "of%d" % ((i + 1) % 2)
+            act(T[base][:], T.gg[:, cur + 16:cur + 16 + NL], ACT.Identity, [("gg", cur + 16, cur + 16 + NL)] + cc(1), [(base, 0, NL)], bias=col(1))
+            aside[i]()
+            flip(0, "gg", cur + 16, WIDE)
+            flip(WIDE, "gg", cur, WIDE)
+            if i == 0:
+                tts(T.dl[:, 2:64:4], T.fa[:], -2.0, 1.0, A.mult, A.add, [("fa", 0, 16)], [("dl", 0, 64)])
+            drip(1)
+            wrapped(of, 0, 1, 6, 1.0, float(LESS))
             for j in range(rad - 1):
-                ttt(T.gg[:, nxt + 16:nxt + 336], T.gg[:, cur + 16:cur + 336].indirect(T[of][:, 0:20]), T[base][:], A.min,
-                    [("gg", cur + 16, cur + 336), (of, 0, 20), (base, 0, C)], [("gg", nxt + 16, nxt + 336)])
+                if i == 2 and j == 0:
+                    ttt(T.dat[:, 2:64:4], T.fa[:], T.c2[:], A.add, [("fa", 0, 16), ("c2", 0, 16)], [("dat", 0, 64)])
+                else:
+                    drip(1)
+                ttt(T.gg[:, nxt + 16:nxt + 16 + NL], T.gg[:, cur + 16:cur + 16 + NL].indirect(T[of][:, 0:NB]), T[base][:], A.min,
+                    [("gg", cur + 16, cur + 16 + NL), (of, 0, 16), (base, 0, NL)], [("gg", nxt + 16, nxt + 16 + NL)])
                 cur, nxt = nxt, cur
-            turn(cur)
-            if i + 1 < len(RADIX):
-                base = "bs%d" % (1 + i % 2)
-                op("a", lambda e: e.activation(T[base][:], T.gg[:, cur + 16:cur + 336], ACT.Identity, bias=col(1)),
-                   [("gg", cur + 16, cur + 336)] + cc(1), [(base, 0, C)])
-                op("a", lambda e: e.activation(T["yi%d" % r][:, C * i:C * i + C], T["yp%d" % r][:, C * i:C * i + C], ACT.Copy),
-                   [("yp%d" % r, C * i, C * i + C)], [("yi%d" % r, C * i, C * i + C)])
-                wrapped("of%d" % ((i + 1) % 2), 0, 1.0, 160.0)
-        for c, ct, sl in ((4, "ct1", 0), (2, "ct0", 1)):
-            ttt(T.dat[:, sl:64:4], TT.indirect(T.sel[:, c:c + 1]), T[ct][:], A.is_equal,
-                [("tt", 0, 672), ("sel", c, c + 1), (ct, 0, 16)], [("dat", 0, 64)])
+        turn("gg", cur, 192, lambda: op("v", lambda e: e.tensor_copy(T.gg[:, cur + 16 + NL:cur + 336], T.gg[:, cur + 16:cur + 16 + NL].indirect(T.ofs[:, 0:NS // 16])),
+                                        [("gg", cur + 16, cur + 16 + NL), ("ofs", 0, 16)], [("gg", cur + 16 + NL, cur + 336)]))
+        drip(len(later))
+        for c, ct, sl in ((10, "ct1", 0), (8, "ct0", 1)):
+            ttt(T.dat[:, sl:64:4], TT.indirect(T.sel[:, c:c + 1]), T[ct][:], A.is_equal, [TN, SE, (ct, 0, 16)], [("dat", 0, 64)])
         op("v", lambda e: e.tensor_tensor_scan(T.sc[:], T.dl[:], T.dat[:], 0.0, A.mult, A.add), [("dl", 0, 64), ("dat", 0, 64)], [("sc", 0, 64)])
         tof = "tof%d" % r
         for h in range(2):
             tts(T[tof][:, 10 * h:10 * h + 10], T.sc[:, 2 + h:39 + h:4], 160.0, None, A.add, None, [("sc", 0, 64)], [(tof, 10 * h, 10 * h + 10)])
 
-    def pairs(r, a, b):
-        for t in range(4):
+    def pairs(r, a, b, some):
+        for t in some:
             yp, yi, tof = "yp%d" % r, "yi%d" % r, "tof%d" % r
             ttt(T["zt%d" % r][:, 4 * a + t:4 * b:4], T[yp][:, C * t:C * t + C].indirect(T[tof][:, a // 16:b // 16]),
                 T[yi][:, C * t + a:C * t + b], A.add, [(yp, C * t, C * t + C), (yi, C * t + a, C * t + b), (tof, a // 16, b // 16)], [("zt%d" % r, 4 * a, 4 * b)])
@@ -309,8 +418,8 @@ def rank_program(g, core, T, topo):
 
     def keep(r, a, bk):
         for b in range(4):
-            op("a", lambda e: e.activation(T["ht%d" % r][:, 4 * a + b:4 * a + 512:4], T.ps[:, 512 * (bk + b):512 * (bk + b) + 128], ACT.Copy, scale=0.03125),
-               [bank(bk + b)], [("ht%d" % r, 4 * a, 4 * a + 512)])
+            act(T["ht%d" % r][:, 4 * a + b:4 * a + 512:4], T.ps[:, 512 * (bk + b):512 * (bk + b) + 128], ACT.Copy,
+                [bank(bk + b)], [("ht%d" % r, 4 * a, 4 * a + 512)], scale=0.03125)
 
     def ship(r, i):
         a = 128 * i
@@ -326,16 +435,12 @@ def rank_program(g, core, T, topo):
         for b in range(4):
             mul(bk + b, 128, "eq", "ep", 128 * b, "rq%d" % r, "rs%d" % r, a, a + 128)
         for b in range(4):
-            o, p = T["bp%d" % r][:, C * b + a:C * b + a + 128], T.ps[:, 512 * (bk + b):512 * (bk + b) + 128]
-            w = [("bp%d" % r, C * b + a, C * b + a + 128)]
-            if b % 2 == 0:
-                op("v", lambda e: e.tensor_copy(o, p), [bank(bk + b)], w)
-            else:
-                op("a", lambda e: e.activation(o, p, ACT.Copy), [bank(bk + b)], w)
+            act(T["bp%d" % r][:, C * b + a:C * b + a + 128], T.ps[:, 512 * (bk + b):512 * (bk + b) + 128], ACT.Copy,
+                [bank(bk + b)], [("bp%d" % r, C * b + a, C * b + a + 128)])
 
-    def advance(r, i):
+    def advance(r, i, some):
         a, b = PARTS[i]
-        for t in range(4):
+        for t in some:
             bp, kof = "bp%d" % r, "kof%d" % (r + 1)
             ttt(T["xt%d" % (r + 1)][:, 4 * a + t:4 * b:4], T[bp][:, C * t:C * t + C].indirect(T[kof][:, a // 16:b // 16]),
                 T["xt%d" % r][:, 4 * a + t:4 * b:4], A.add,
@@ -343,35 +448,39 @@ def rank_program(g, core, T, topo):
 
     for r in range(ROUNDS):
         register(r)
+        if r == 0:
+            fetch(0)
         nr = 352 * (2 + r)
         kr, kk, kof, tof = C * r, "kk%d" % r, "kof%d" % r, "tof%d" % r
-        op("a", lambda e: e.activation(T[kk][:], T.krs[:, kr:kr + C].indirect(T[kof][:, 0:20]), ACT.Copy),
-           [("krs", kr, kr + C), (kof, 0, 20)], [(kk, 0, C)])
-        op("a", lambda e: e.activation(T.gg[:, nr + 16:nr + 336], T[kk][:, 0:C].indirect(T[tof][:, 0:20]), ACT.Copy),
-           [(kk, 0, C), (tof, 0, 20)], [("gg", nr + 16, nr + 336)])
+        act(T[kk][:], T.krs[:, kr:kr + C].indirect(T[kof][:, 0:20]), ACT.Copy, [("krs", kr, kr + C), (kof, 0, 20)], [(kk, 0, C)])
+        act(T.gg[:, nr + 16:nr + 336], T[kk][:, 0:C].indirect(T[tof][:, 0:20]), ACT.Copy, [(kk, 0, C), (tof, 0, 20)], [("gg", nr + 16, nr + 336)])
         zq, zs, zt = "zq%d" % r, "zs%d" % r, "zt%d" % r
+        pairs(r, 0, 128, range(4))
         for i in range(2):
-            pairs(r, 128 * i, 128 * i + 128)
+            nxt = (128, 256) if i == 0 else (CROSS, C)
+            pairs(r, nxt[0], nxt[1], [0])
             quant(zq, zs, 128 * i, 128 * i + 128, zt, 512 * i, 512 * i + 512)
             layer(r, 128 * i, 4 * i)
             keep(r, 128 * i, 4 * i)
+            pairs(r, nxt[0], nxt[1], [1, 2, 3] if i == 0 else [1, 2])
         ship(r, 0)
-        pairs(r, CROSS, C)
+        pairs(r, CROSS, C, [3])
+        ship(r, 1)
         quant(zq, zs, 256, 384, zt, 4 * 192, 4 * C)
         layer(r, 256, 0)
         for b in range(4):
-            op("a", lambda e: e.activation(T["bp%d" % r][:, C * b + CROSS:C * b + C], T.ps[:, 512 * b + 64:512 * b + 128], ACT.Copy, scale=0.03125),
-               [bank(b)], [("bp%d" % r, C * b + CROSS, C * b + C)])
-        ship(r, 1)
-        turn(nr)
-        wrapped("kof%d" % (r + 1), 0, 1.0, 160.0)
+            act(T["bp%d" % r][:, C * b + CROSS:C * b + C], T.ps[:, 512 * b + 64:512 * b + 128], ACT.Copy,
+                [bank(b)], [("bp%d" % r, C * b + CROSS, C * b + C)], scale=0.03125)
+        turn("gg", nr, HALF)
+        wrapped("kof%d" % (r + 1), 0, 2, 0, 1.0, 160.0)
         if r + 1 < ROUNDS:
             k4 = "k4%d" % (r + 1)
             for t in range(4):
-                wrapped(k4, 32 * t, 4.0, 640.0 + t)
+                wrapped(k4, 32 * t, 2, 0, 4.0, 640.0 + t)
             dma("s", "dk%d" % (r + 1), [(T["lk%d" % (r + 1)][:, :], T.gg[0:128:16, nr + 16:nr + 336],
                                          [("gg", nr + 16, nr + 336)], [("lk%d" % (r + 1), 0, 160)])])
             share(r + 1)
+            fetch(r + 1)
         else:
             tts(T.kpf[:], T.gg[:, nr + 16:nr + 336], 160.0, None, A.add, None, [("gg", nr + 16, nr + 336)], [("kpf", 0, C)])
             dma("s", "okp", [(T.kp[:, :], T.kpf[0:128:16, :], [("kpf", 0, C)], [])])
@@ -381,22 +490,24 @@ def rank_program(g, core, T, topo):
         unpack(r, 0, 4)
         unpack(r, 1, 0)
         n = r + 1
+        advance(r, 0, range(4))
+        advance(r, 1, [0])
         if n < ROUNDS:
-            advance(r, 0)
             qstate(n, 0)
             score(n, 0)
-            advance(r, 1)
-            sign(0)
+            advance(r, 1, [1, 2, 3])
             qstate(n, 1)
             score(n, 1)
+            sign(0)
             sign(1)
         else:
             for i in range(2):
                 a, b = PARTS[i]
-                advance(r, i)
+                if i == 1:
+                    advance(r, 1, [1, 2, 3])
                 qstate(n, i)
                 mul(4 + i, b - a, "vq", "vs", 0, "xq%d" % n, "xs%d" % n, a, b)
-                op("a", lambda e: e.activation(T.yo[:, a:b], T.ps[:, 512 * (4 + i):512 * (4 + i) + b - a], ACT.Copy), [bank(4 + i)], [("yo", a, b)])
+                act(T.yo[:, a:b], T.ps[:, 512 * (4 + i):512 * (4 + i) + b - a], ACT.Copy, [bank(4 + i)], [("yo", a, b)])
                 dma("s", "oc%d" % i, [(T.oc[:, 4 * a:4 * b], T["xq%d" % n][:, a:b].bitcast(dt.uint8), [("xq%d" % n, a, b)], [])])
                 dma("a", "oy%d" % i, [(T.y[:, a:b], T.yo[:, a:b], [("yo", a, b)], [])])
             dma("s", "os", [(T.osc[4 * i:4 * i + 4, :], T["xs%d" % n][32 * i:32 * i + 4, :], [("xs%d" % n, 0, C)], []) for i in range(4)])

from concourse.mybir import dt, AluOpType, ActivationFunctionType

C, HALF, CROSS = 320, 160, 256
ROUNDS = 3
MASKS = [1, 2, 3]
LONG = [(0, 2), (4, 8), (11, 12), (14, 20)]
SHORT = [(2, 4), (8, 11), (12, 14)]
BLOCKS = [b for a, e in LONG + SHORT for b in range(a, e)]
AT = {b: i for i, b in enumerate(BLOCKS)}
NB = sum(e - a for a, e in LONG)
NL, NS = 16 * NB, C - 16 * NB
RADIX = [3, 3, 3, 3, 3]
BIG, LESS = 1024.0, 256
G0 = NL + 16
F32, BF, I32, U16, F8, U8 = "float32", "bfloat16", "int32", "uint16", "float8_e4m3fn_x4", "uint8"

SCRATCH = {
    "ub": ("sbuf", [128, 512], BF), "vb": ("sbuf", [128, 512], BF),
    "uq": ("sbuf", [128, 128], F8), "us": ("sbuf", [128, 128], U8),
    "vq": ("sbuf", [128, 128], F8), "vs": ("sbuf", [128, 128], U8),
    "wq": ("sbuf", [128, 512], F8), "wp": ("sbuf", [128, 512], U8),
    "one": ("sbuf", [128, 512], BF), "eb": ("sbuf", [128, 2048], BF),
    "eq": ("sbuf", [128, 512], F8), "ep": ("sbuf", [128, 512], U8),
    "pidx": ("sbuf", [128, 1], I32), "qidx": ("sbuf", [128, 1], I32), "grp": ("sbuf", [128, 1], I32),
    "yrow": ("sbuf", [128, C], F32), "cwi": ("sbuf", [128, 16], F32), "cst": ("sbuf", [128, 16], F32), "sel": ("sbuf", [128, 12], U16),
    "rt": ("sbuf", [128, 128], F32), "ru": ("sbuf", [128, 128], F32), "ki": ("sbuf", [128, 5], I32), "kf": ("sbuf", [128, 5], F32),
    "dr": ("sbuf", [128, HALF], F32), "d1": ("sbuf", [128, HALF], F32), "k1b": ("sbuf", [128, HALF], F32), "k3b": ("sbuf", [128, HALF], F32),
    "k1": ("sbuf", [128, HALF], BF), "k3": ("sbuf", [128, HALF], F32), "bs0": ("sbuf", [128, NL], BF),
    "cw": ("sbuf", [128, 16], F32), "ca": ("sbuf", [128, 16], F32), "cb": ("sbuf", [128, 16], F32), "cd": ("sbuf", [128, 16], F32),
    "c2": ("sbuf", [128, 16], F32), "ct0": ("sbuf", [128, 16], F32), "ct1": ("sbuf", [128, 16], F32),
    "dl": ("sbuf", [128, 64], F32), "dat": ("sbuf", [128, 64], F32), "sc": ("sbuf", [128, 64], F32),
    "fi": ("sbuf", [128, 16], I32), "fa": ("sbuf", [128, 16], I32),
    "kli": ("sbuf", [128, 20], I32), "klb": ("sbuf", [128, 32], BF), "klt": ("sbuf", [128, 32], BF),
    "w0": ("sbuf", [128, G0 + C + 16], BF), "gg": ("sbuf", [128, 5 * 352], BF), "krs": ("sbuf", [128, 3 * C], BF),
    "bits": ("sbuf", [128, C], BF), "bs1": ("sbuf", [128, NL], BF), "bs2": ("sbuf", [128, NL], BF),
    "tt": ("sbuf", [128, 864], BF), "of0": ("sbuf", [128, 16], U16), "of1": ("sbuf", [128, 16], U16), "ofs": ("sbuf", [128, 16], U16),
    "kpf": ("sbuf", [128, C], F32), "yo": ("sbuf", [128, C], F32),
    "ps": ("psum", [128, 4096], F32),
}
for _r in range(ROUNDS + 1):
    SCRATCH["xt%d" % _r] = ("sbuf", [128, 4 * C], BF)
    SCRATCH["xq%d" % _r] = ("sbuf", [128, C], F8)
    SCRATCH["xs%d" % _r] = ("sbuf", [128, C], U8)
    SCRATCH["kof%d" % _r] = ("sbuf", [128, 32], U16)
for _r in range(ROUNDS):
    SCRATCH["k4%d" % _r] = ("sbuf", [128, 128], U16)
    SCRATCH["tof%d" % _r] = ("sbuf", [128, 20], U16)
    SCRATCH["kk%d" % _r] = ("sbuf", [128, C], BF)
    SCRATCH["yp%d" % _r] = ("sbuf", [128, 4 * C], BF)
    SCRATCH["yi%d" % _r] = ("sbuf", [128, 4 * C], BF)
    SCRATCH["zt%d" % _r] = ("sbuf", [128, 4 * C], BF)
    SCRATCH["zq%d" % _r] = ("sbuf", [128, 384], F8)
    SCRATCH["zs%d" % _r] = ("sbuf", [128, 384], U8)
    SCRATCH["ht%d" % _r] = ("sbuf", [128, 4 * CROSS], BF)
    SCRATCH["hq%d" % _r] = ("sbuf", [128, CROSS], F8)
    SCRATCH["hs%d" % _r] = ("sbuf", [128, CROSS], U8)
    SCRATCH["rq%d" % _r] = ("sbuf", [128, CROSS], F8)
    SCRATCH["rs%d" % _r] = ("sbuf", [128, CROSS], U8)
    SCRATCH["bp%d" % _r] = ("sbuf", [128, 4 * C], BF)
    SCRATCH["lk%d" % _r] = ("dram", [128, 20], BF)
    SCRATCH["rk%d" % _r] = ("dram", [128, 20], BF)
SEMAPHORES = ["sv", "sa", "sp", "sg", "sent", "lx0", "lx1", "lu", "lv", "lk", "lwc", "lws",
              "oc0", "oc1", "os", "oy0", "oy1", "okp"]
for _r in range(ROUNDS):
    SEMAPHORES += ["dk%d" % _r, "dr%d" % _r, "arl%d" % _r, "ar0%d" % _r, "ar1%d" % _r]


def rank_program(g, core, T, topo):
    rank = T.rank_of(core)
    if rank is None:
        return
    A, ACT = AluOpType, ActivationFunctionType
    queue = {"v": g.vector, "a": g.scalar, "p": g.tensor, "g": g, "s": g.sync}
    own = {"v": "sv", "a": "sa", "p": "sp", "g": "sg"}
    total, seen, hist = {}, {q: {} for q in queue}, {}

    def need(q, reads, writes, compute):
        deps = {}
        for (names, isw) in ((reads, False), (writes, True)):
            for (b, lo, hi) in names:
                for (l, h, w, eq, sem, val) in hist.get(b, []):
                    if l < hi and lo < h and (w or isw):
                        if compute and eq == q and isw:
                            continue
                        deps[sem] = max(deps.get(sem, 0), val)
        for sem in deps:
            if seen[q].get(sem, 0) < deps[sem]:
                queue[q].wait_ge(T.sem[sem], deps[sem])
                seen[q][sem] = deps[sem]

    def note(q, reads, writes, sem, val):
        for (b, lo, hi) in writes:
            hist[b] = [e for e in hist.get(b, []) if not (lo <= e[0] and e[1] <= hi and (e[3] != q or e[2] is False or (lo, hi) == (e[0], e[1])))]
            hist[b].append((lo, hi, True, q, sem, val))
        for (b, lo, hi) in reads:
            keep = [e for e in hist.get(b, []) if not (not e[2] and e[3] == q and lo <= e[0] and e[1] <= hi)]
            keep.append((lo, hi, False, q, sem, val))
            hist[b] = keep

    def op(q, call, reads, writes):
        need(q, reads, writes, True)
        sem = own[q]
        total[sem] = total.get(sem, 0) + 1
        call(queue[q]).then_inc(T.sem[sem], 1)
        note(q, reads, writes, sem, total[sem])

    def dma(q, sem, pairs):
        for (out, in_, reads, writes) in pairs:
            need(q, reads, writes, False)
        for (out, in_, reads, writes) in pairs:
            total[sem] = total.get(sem, 0) + 16
            queue[q].dma_start(out, in_).then_inc(T.sem[sem], 16)
        for (out, in_, reads, writes) in pairs:
            note("d" + q, reads, writes, sem, total[sem])

    def send(dst, out, in_, reads, sem):
        need("g", reads, [], False)
        rid, pid = topo.addr(dst)[0], topo.addr(dst)[1]
        n = len(topo.engines(core, dst))
        g.remote_dma(out, in_, T.sem[sem], T.sem.sent, pid, rid, topo.mask(core, dst))
        total["sent"] = total.get("sent", 0) + n
        total[sem] = total.get(sem, 0) + n

    def tts(out, in0, s1, s2, o0, o1, reads, writes):
        if o1 is None:
            op("v", lambda e: e.tensor_scalar(out, in0, s1, None, o0), reads, writes)
        else:
            op("v", lambda e: e.tensor_scalar(out, in0, s1, s2, o0, o1), reads, writes)

    def ttt(out, in0, in1, o, reads, writes):
        op("v", lambda e: e.tensor_tensor(out, in0, in1, o), reads, writes)

    def act(out, in_, f, reads, writes, **k):
        op("a", lambda e: e.activation(out, in_, f, **k), reads, writes)

    def quant(q, s, a, b, t, ta, tb):
        op("v", lambda e: e.quantize_mx(T[q][:, a:b], T[s][:, a:b], T[t][:, ta:tb]), [(t, ta, tb)], [(q, a, b), (s, a, b)])

    def bank(i):
        return ("ps", 512 * i, 512 * i + 512)

    def mul(i, n, lq, ls, l, rq, rs, a, b):
        op("p", lambda e: e.matmul_mx(T.ps[:, 512 * i:512 * i + n], T[lq][:, l:l + 128], T[ls][:, l:l + 128],
                                      T[rq][:, a:b], T[rs][:, a:b], True, True),
           [(lq, l, l + 128), (ls, l, l + 128), (rq, a, b), (rs, a, b)], [bank(i)])

    peer = [T.cores[rank ^ m] for m in MASKS]
    dma("s", "lx0", [(T.xt0[:, 0:768], T.x[:, 0:768], [], [("xt0", 0, 768)])])
    dma("a", "lk", [(T.kli[:], T.kl[:, :], [], [("kli", 0, 20)])])
    dma("s", "lx1", [(T.xt0[:, 768:1280], T.x[:, 768:1280], [], [("xt0", 768, 1280)])])
    dma("a", "lu", [(T.ub[:], T.u[:, :], [], [("ub", 0, 512)])])
    dma("s", "lwc", [(T.wq[:, 0:512].bitcast(dt.uint8), T.wc[:, 0:2048], [], [("wq", 0, 512)])])
    dma("s", "lws", [(T.wp[:, 0:512], T.ws[:, 0:512], [], [("wp", 0, 512)])])
    dma("a", "lv", [(T.vb[:], T.v[:, :], [], [("vb", 0, 512)])])

    later = []

    def drip(n):
        for call in later[:n]:
            call()
        later[:n] = []

    def col(i):
        return T.cst[:, i:i + 1]

    def cc(*i):
        return [("cst", j, j + 1) for j in i]

    def scol(i, in0, names, s1, s2, o0, o1):
        tts(col(i), in0, s1, s2, o0, o1, names, cc(i))
    P1, Q1, GR, YR = ("pidx", 0, 1), ("qidx", 0, 1), ("grp", 0, 1), ("yrow", 0, C)
    op("g", lambda e: e.iota(T.pidx[:], [[0, 1]], 0, 1), [], [P1])
    op("g", lambda e: e.iota(T.yrow[:], [[1, C]], 0, 0, allow_small_or_imprecise_dtypes=True), [], [YR])
    op("g", lambda e: e.iota(T.cwi[:], [[16, 16]], 0, 1, allow_small_or_imprecise_dtypes=True), [], [("cwi", 0, 16)])
    op("v", lambda e: e.memset(T.rt[:], 0.0), [], [("rt", 0, 128)])
    op("v", lambda e: e.memset(T.one[:], 1.0), [], [("one", 0, 512)])
    op("v", lambda e: e.memset(T.klb[:], 0.0), [], [("klb", 0, 32)])
    cuts = sorted([(a, e, 16 * (AT[a] - a)) for a, e in LONG] + [(a, e, G0) for a, e in SHORT])
    for a, e, d in cuts:
        op("v", lambda x: x.memset(T.dr[:, 8 * a:8 * e], float(d)), [], [("dr", 8 * a, 8 * e)])
    tts(T.qidx[:], T.pidx[:], 15, None, A.bitwise_and, None, [P1], [Q1])
    tts(T.grp[:], T.pidx[:], 4, None, A.arith_shift_right, None, [P1], [GR])
    scol(0, T.qidx[:], [Q1], 0.0, None, A.is_equal, None)
    scol(1, T.qidx[:], [Q1], 0.0, BIG, A.is_equal, A.mult)
    scol(8, T.grp[:], [GR], 1.0, None, A.mult, None)
    scol(9, T.grp[:], [GR], 16.0, None, A.mult, None)
    scol(2, col(0), cc(0), 1.0, None, A.add, None)
    scol(3, col(0), cc(0), float(-LESS), None, A.mult, None)
    scol(4, col(0), cc(0), 2.0, 2.0, A.mult, A.add)
    scol(5, col(0), cc(0), float(1 - 2 * LESS - HALF), float(HALF), A.mult, A.add)
    scol(6, col(0), cc(0), -LESS - BIG, BIG, A.mult, A.add)

    def widen(nm, a, b, src, c, scale, bias, names):
        act(T[nm][:, a:b], T[src][:, c:c + b - a], ACT.Identity, [(src, c, c + b - a)] + names, [(nm, a, b)], bias=bias, scale=scale)

    def blank(nm, a, b):
        act(T[nm][:, a:b], T.yrow[:, 0:b - a], ACT.Copy, [YR], [(nm, a, b)], scale=0.0)
    lists = [LONG, SHORT]
    for h in (0, 10):
        runs = []
        for b in range(h, h + 10):
            if runs and AT[b] == runs[-1][1]:
                runs[-1][1] += 1
            else:
                runs.append([AT[b], AT[b] + 1])
        lists.append(runs)

    def row_of(i):
        for j in (32 * i, 32 * i + 16):
            for a, e in lists[i]:
                w = ("rt", j, j + e - a)
                if i < 2:
                    act(T.rt[:, j:j + e - a], T.yrow[:, a:e], ACT.Copy, [YR, w], [w])
                else:
                    op("g", lambda x: x.iota(T.rt[:, j:j + e - a], [[1, e - a]], a, 0, allow_small_or_imprecise_dtypes=True), [w], [w])
                j += e - a
    row_of(2)
    row_of(3)
    widen("k1b", 0, HALF, "yrow", 0, col(2), col(3), cc(2, 3))
    widen("d1", 0, HALF, "dr", 0, col(0), 0.0, cc(0))
    widen("k3b", 0, HALF, "yrow", 0, col(4), col(5), cc(4, 5))
    row_of(0)
    row_of(1)
    blank("tt", 672, 864)
    ttt(T.k1[:], T.k1b[:], T.d1[:], A.add, [("k1b", 0, HALF), ("d1", 0, HALF)], [("k1", 0, HALF)])
    tts(T.d1[:], T.d1[:], 2.0, None, A.mult, None, [("d1", 0, HALF)], [("d1", 0, HALF)])
    KL = [("kli", 0, 20)]
    tts(T.klb[:, 0:20], T.kli[:], -160.0, None, A.add, None, KL, [("klb", 0, 20)])
    tts(T.kof0[:, 0:20], T.kli[:], 0.0, None, A.add, None, KL, [("kof0", 0, 20)])
    ttt(T.k3[:], T.k3b[:], T.d1[:], A.add, [("k3b", 0, HALF), ("d1", 0, HALF)], [("k3", 0, HALF)])
    op("v", lambda e: e.transpose(T.klt[:], T.klb[:]), [("klb", 0, 32)], [("klt", 0, 32)])
    WIDE = 32 * ((NB + 1) // 2)
    RU, KI, KF = [("ru", 0, 128)], [("ki", 0, 4)], [("kf", 0, 4)]
    KQ = [("ki", 4, 5), ("kf", 4, 5)]

    def seln(o, in0, s1, s2, o0, o1, names):
        tts(o, in0, s1, s2, o0, o1, names, [("sel", 0, 12)])
    tts(T.ki[:, 4:5], T.qidx[:], col(8), None, A.add, None, [Q1] + cc(8), [("ki", 4, 5)])
    tts(T.kf[:, 4:5], T.qidx[:], 16.0, None, A.mult, None, [Q1], [("kf", 4, 5)])

    def own_places():
        tts(T.ki[:, 4:5], T.ki[:, 4:5], 1, None, A.bitwise_and, None, [("ki", 4, 5)], [("ki", 4, 5)])
        for t in range(4):
            tts(T.k40[:, 32 * t:32 * t + 20], T.kli[:], 4.0, float(t), A.mult, A.add, KL, [("k40", 32 * t, 32 * t + 20)])
        seln(T.sel[:, 6:7], T.ki[:, 4:5], float(WIDE + 16), T.kf[:, 4:5], A.mult, A.add, KQ)
        seln(T.sel[:, 0:1], T.ki[:, 4:5], float(C + 16), T.kf[:, 4:5], A.mult, A.add, KQ)

    where = [
        lambda: op("v", lambda e: e.transpose(T.ru[:], T.rt[:]), [("rt", 0, 128)], RU),
        lambda: (tts(T.ki[:, 0:4], T.ru[:, 0:128:32], col(8), None, A.add, None, RU + cc(8), KI),
                 tts(T.kf[:, 0:4], T.ru[:, 0:128:32], 16.0, None, A.mult, None, RU, KF)),
        lambda: tts(T.ki[:, 0:4], T.ki[:, 0:4], 1, None, A.bitwise_and, None, KI, KI),
        lambda: tts(T.ki[:, 0:4], T.ki[:, 0:4], C + 16, None, A.mult, None, KI, KI),
        lambda: ttt(T.kf[:, 0:4], T.kf[:, 0:4], T.ki[:, 0:4], A.add, KI + KF, KF),
        lambda: seln(T.sel[:, 2:6:2], T.kf[:, 0:2], 0.0, None, A.add, None, KF)]

    def find(i):
        where[i]()
    later += [lambda: seln(T.sel[:, 8:12:2], T.kf[:, 2:4], 1.0, None, A.add, None, KF),
              lambda: seln(T.sel[:, 1:2], T.sel[:, 0:1], 256.0, None, A.add, None, [("sel", 0, 12)])]
    SE = ("sel", 0, 12)
    for a, e in LONG:
        widen("bs0", 16 * AT[a], 16 * (AT[a] + e - a), "yrow", 16 * a, 1.0, col(1), cc(1))
    widen("w0", 0, NL, "yrow", 0, col(0), col(6), cc(0, 6))
    blank("w0", NL, G0)
    blank("w0", G0 + C, G0 + C + 16)
    for i in range(2):
        blank("gg", 352 * i, 352 * i + 16)
        blank("gg", 352 * i + 16 + NL, 352 * i + 352)
    CW = [("cw", 0, 16)]
    later += [
        lambda: tts(T.cw[:], T.cwi[:], col(9), None, A.subtract, None, [("cwi", 0, 16)] + cc(9), CW),
        lambda: op("v", lambda e: e.memset(T.dl[:, 0:64:4], 0.0), [], [("dl", 0, 64)]),
        lambda: tts(T.c2[:], T.cw[:], 2.0, -160.0, A.mult, A.add, CW, [("c2", 0, 16)]),
        lambda: op("v", lambda e: e.memset(T.dl[:, 3:64:4], -1.0), [], [("dl", 0, 64)]),
        lambda: tts(T.dat[:, 3:64:4], T.cw[:], 4.0, -319.0, A.mult, A.add, CW, [("dat", 0, 64)]),
        lambda: tts(T.ca[:], T.cw[:], 0.0, None, A.is_equal, None, CW, [("ca", 0, 16)]),
        lambda: tts(T.dl[:, 1:64:4], T.cw[:], 159.0, 2.0, A.is_equal, A.mult, CW, [("dl", 0, 64)]),
        lambda: tts(T.cb[:], T.cw[:], 159.0, -160.0, A.is_equal, A.mult, CW, [("cb", 0, 16)]),
        lambda: ttt(T.ca[:], T.cw[:], T.ca[:], A.subtract, CW + [("ca", 0, 16)], [("ca", 0, 16)]),
        lambda: tts(T.dl[:, 1:64:4], T.dl[:, 1:64:4], -1.0, None, A.add, None, [("dl", 0, 64)], [("dl", 0, 64)]),
        lambda: tts(T.cd[:], T.cw[:], 159.0, 161.0, A.is_equal, A.mult, CW, [("cd", 0, 16)]),
        lambda: ttt(T.ct0[:], T.ca[:], T.cb[:], A.add, [("ca", 0, 16), ("cb", 0, 16)], [("ct0", 0, 16)]),
        lambda: ttt(T.ct1[:], T.ca[:], T.cd[:], A.add, [("ca", 0, 16), ("cd", 0, 16)], [("ct1", 0, 16)])]

    dma("s", "dk0", [(T.lk0[16 * i:16 * i + 16, :], T.klt[32 * (i // 2):32 * (i // 2) + 20, 16 * (i % 2):16 * (i % 2) + 16],
                      [("klt", 0, 32)], [("lk0", 20 * i, 20 * i + 20)]) for i in range(8)])

    def share(r):
        send(peer[r], T["rk%d" % r][:, :], T["lk%d" % r][:, :], [("lk%d" % r, 0, 160)], "arl%d" % r)
        note("net", [], [("rk%d" % r, 0, 160)], "arl%d" % r, total["arl%d" % r])

    def fetch(r):
        dma("s", "dr%d" % r, [(T.krs[0:128:16, C * r:C * r + C], T["rk%d" % r][:, :],
                               [("rk%d" % r, 0, 160)], [("krs", C * r, C * r + C)])])

    share(0)
    for b in range(4):
        op("g", lambda e: e.affine_select(T.eb[:, 512 * b:512 * b + 512], T.one[:], [[1, 512]], A.is_equal, 0.0, -b, -4),
           [("one", 0, 512)], [("eb", 512 * b, 512 * b + 512)])

    def flip(to, nm, c, n):
        op("v", lambda e: e.transpose(T.tt[:, to:to + n], T[nm][:, c:c + n]), [(nm, c, c + n)], [("tt", to, to + n)])

    def turn(nm, c0, cut, ahead=None, between=None):
        if ahead is not None:
            ahead()
        flip(0, nm, c0 + 16, cut)
        flip(C, nm, c0, cut)
        if between is not None:
            between()
        flip(cut, nm, c0 + 16 + cut, C - cut)
        flip(C + cut, nm, c0 + cut, C + 32 - cut)

    TT, TN = T.tt[:, 0:864], ("tt", 0, 864)

    def wrapped(nm, a, wide, sel, by, plus):
        tts(T[nm][:, a:a + 16 * wide], TT.indirect(T.sel[:, sel:sel + wide]), by, plus, A.mult, A.add,
            [TN, SE], [(nm, a, a + 16 * wide)])

    PARTS = [(0, 192), (192, C)]

    def qstate(r, i):
        a, b = PARTS[i]
        quant("xq%d" % r, "xs%d" % r, a, b, "xt%d" % r, 4 * a, 4 * b)

    def score(r, i):
        a, b = PARTS[i]
        mul(4 + i, b - a, "uq", "us", 0, "xq%d" % r, "xs%d" % r, a, b)

    def sign(i):
        a, b = PARTS[i]
        tts(T.bits[:, a:b], T.ps[:, 512 * (4 + i):512 * (4 + i) + b - a], 0.0, col(0), A.is_gt, A.mult, [bank(4 + i)] + cc(0), [("bits", a, b)])

    quant("uq", "us", 0, 128, "ub", 0, 512)
    for i in range(2):
        qstate(0, i)
        score(0, i)
    own_places()
    for i in range(2):
        find(i)
        sign(i)

    def register(r):
        kof = "kof%d" % r
        H1 = G0 + HALF
        ttt(T.w0[:, G0:H1], T.bits[:, 0:C].indirect(T[kof][:, 0:10]), T.k1[:], A.add,
            [("bits", 0, C), (kof, 0, 10), ("k1", 0, HALF)], [("w0", G0, H1)])

        def half(t):
            act(T["yp%d" % r][:, C * t:C * t + C], T["xt%d" % r][:, 0:4 * C].indirect(T["k4%d" % r][:, 32 * t:32 * t + 20]), ACT.Copy,
                [("xt%d" % r, 0, 4 * C), ("k4%d" % r, 32 * t, 32 * t + 20)], [("yp%d" % r, C * t, C * t + C)], scale=0.5)

        def again(t):
            act(T["yi%d" % r][:, C * t:C * t + C], T["yp%d" % r][:, C * t:C * t + C], ACT.Copy,
                [("yp%d" % r, C * t, C * t + C)], [("yi%d" % r, C * t, C * t + C)])

        def blanks(i):
            if r == 0:
                blank("gg", 352 * i + 704, 352 * i + 720)
                blank("gg", 352 * i + 1040, 352 * i + 1056)
                blank("krs", C * i, C * i + C)
        half(0)
        half(1)
        aside = [lambda: half(2), lambda: (half(3), again(0)), lambda: (again(1), again(2), blanks(0)),
                 lambda: (again(3), blanks(1)), lambda: blanks(2)]
        gap = find if r == 0 else (lambda i: None)
        gap(2)
        ttt(T.w0[:, H1:G0 + C], T.k3[:], T.w0[:, G0:H1], A.subtract, [("k3", 0, HALF), ("w0", G0, H1)], [("w0", H1, G0 + C)])
        gap(3)
        turn("w0", G0 - 16, HALF, None, lambda: gap(4))
        gap(5)
        wrapped("of0", 0, 1, 2, 1.0, float(LESS))
        wrapped("ofs", 0, 1, 4, 1.0, float(LESS))
        op("v", lambda e: e.tensor_copy(T.fi[:], TT.indirect(T.sel[:, 0:1])), [TN, SE], [("fi", 0, 16)])
        cur, nxt = 352, 0
        ttt(T.gg[:, 16:16 + NL], T.w0[:, 0:G0 + C].indirect(T.of0[:, 0:NB]), T.bs0[:], A.min,
            [("w0", 0, G0 + C), ("of0", 0, 16), ("bs0", 0, NL)], [("gg", 16, 16 + NL)])
        cur, nxt = nxt, cur
        tts(T.fa[:], T.fi[:], 1, None, A.bitwise_and, None, [("fi", 0, 16)], [("fa", 0, 16)])
        for i, rad in enumerate(RADIX):
            base, of = "bs%d" % (1 + i % 2), "of%d" % ((i + 1) % 2)
            act(T[base][:], T.gg[:, cur + 16:cur + 16 + NL], ACT.Identity, [("gg", cur + 16, cur + 16 + NL)] + cc(1), [(base, 0, NL)], bias=col(1))
            aside[i]()
            flip(0, "gg", cur + 16, WIDE)
            flip(WIDE, "gg", cur, WIDE)
            if i == 0:
                tts(T.dl[:, 2:64:4], T.fa[:], -2.0, 1.0, A.mult, A.add, [("fa", 0, 16)], [("dl", 0, 64)])
            drip(1)
            wrapped(of, 0, 1, 6, 1.0, float(LESS))
            for j in range(rad - 1):
                if i == 2 and j == 0:
                    ttt(T.dat[:, 2:64:4], T.fa[:], T.c2[:], A.add, [("fa", 0, 16), ("c2", 0, 16)], [("dat", 0, 64)])
                else:
                    drip(1)
                ttt(T.gg[:, nxt + 16:nxt + 16 + NL], T.gg[:, cur + 16:cur + 16 + NL].indirect(T[of][:, 0:NB]), T[base][:], A.min,
                    [("gg", cur + 16, cur + 16 + NL), (of, 0, 16), (base, 0, NL)], [("gg", nxt + 16, nxt + 16 + NL)])
                cur, nxt = nxt, cur
        turn("gg", cur, 192, lambda: op("v", lambda e: e.tensor_copy(T.gg[:, cur + 16 + NL:cur + 336], T.gg[:, cur + 16:cur + 16 + NL].indirect(T.ofs[:, 0:NS // 16])),
                                        [("gg", cur + 16, cur + 16 + NL), ("ofs", 0, 16)], [("gg", cur + 16 + NL, cur + 336)]))
        drip(len(later))
        for c, ct, sl in ((10, "ct1", 0), (8, "ct0", 1)):
            ttt(T.dat[:, sl:64:4], TT.indirect(T.sel[:, c:c + 1]), T[ct][:], A.is_equal, [TN, SE, (ct, 0, 16)], [("dat", 0, 64)])
        op("v", lambda e: e.tensor_tensor_scan(T.sc[:], T.dl[:], T.dat[:], 0.0, A.mult, A.add), [("dl", 0, 64), ("dat", 0, 64)], [("sc", 0, 64)])
        tof = "tof%d" % r
        for h in range(2):
            tts(T[tof][:, 10 * h:10 * h + 10], T.sc[:, 2 + h:39 + h:4], 160.0, None, A.add, None, [("sc", 0, 64)], [(tof, 10 * h, 10 * h + 10)])

    def pairs(r, a, b, some):
        for t in some:
            yp, yi, tof = "yp%d" % r, "yi%d" % r, "tof%d" % r
            ttt(T["zt%d" % r][:, 4 * a + t:4 * b:4], T[yp][:, C * t:C * t + C].indirect(T[tof][:, a // 16:b // 16]),
                T[yi][:, C * t + a:C * t + b], A.add, [(yp, C * t, C * t + C), (yi, C * t + a, C * t + b), (tof, a // 16, b // 16)], [("zt%d" % r, 4 * a, 4 * b)])

    def layer(r, zcol, bk):
        for b in range(4):
            mul(bk + b, 128, "wq", "wp", 128 * b, "zq%d" % r, "zs%d" % r, zcol, zcol + 128)

    def keep(r, a, bk):
        for b in range(4):
            act(T["ht%d" % r][:, 4 * a + b:4 * a + 512:4], T.ps[:, 512 * (bk + b):512 * (bk + b) + 128], ACT.Copy,
                [bank(bk + b)], [("ht%d" % r, 4 * a, 4 * a + 512)], scale=0.03125)

    def ship(r, i):
        a = 128 * i
        quant("hq%d" % r, "hs%d" % r, a, a + 128, "ht%d" % r, 4 * a, 4 * a + 512)
        sem = "ar%d%d" % (i, r)
        send(peer[r], T["rq%d" % r][:, a:a + 128].bitcast(dt.uint8), T["hq%d" % r][:, a:a + 128].bitcast(dt.uint8), [("hq%d" % r, a, a + 128)], sem)
        send(peer[r], T["rs%d" % r][:, a:a + 128], T["hs%d" % r][:, a:a + 128], [("hs%d" % r, a, a + 128)], sem)

    def unpack(r, i, bk):
        a = 128 * i
        sem = "ar%d%d" % (i, r)
        note("net", [], [("rq%d" % r, a, a + 128), ("rs%d" % r, a, a + 128)], sem, total[sem])
        for b in range(4):
            mul(bk + b, 128, "eq", "ep", 128 * b, "rq%d" % r, "rs%d" % r, a, a + 128)
        for b in range(4):
            act(T["bp%d" % r][:, C * b + a:C * b + a + 128], T.ps[:, 512 * (bk + b):512 * (bk + b) + 128], ACT.Copy,
                [bank(bk + b)], [("bp%d" % r, C * b + a, C * b + a + 128)])

    def advance(r, i, some):
        a, b = PARTS[i]
        for t in some:
            bp, kof = "bp%d" % r, "kof%d" % (r + 1)
            ttt(T["xt%d" % (r + 1)][:, 4 * a + t:4 * b:4], T[bp][:, C * t:C * t + C].indirect(T[kof][:, a // 16:b // 16]),
                T["xt%d" % r][:, 4 * a + t:4 * b:4], A.add,
                [(bp, C * t, C * t + C), (kof, a // 16, b // 16), ("xt%d" % r, 4 * a, 4 * b)], [("xt%d" % (r + 1), 4 * a, 4 * b)])

    for r in range(ROUNDS):
        register(r)
        if r == 0:
            fetch(0)
        nr = 352 * (2 + r)
        kr, kk, kof, tof = C * r, "kk%d" % r, "kof%d" % r, "tof%d" % r
        act(T[kk][:], T.krs[:, kr:kr + C].indirect(T[kof][:, 0:20]), ACT.Copy, [("krs", kr, kr + C), (kof, 0, 20)], [(kk, 0, C)])
        act(T.gg[:, nr + 16:nr + 336], T[kk][:, 0:C].indirect(T[tof][:, 0:20]), ACT.Copy, [(kk, 0, C), (tof, 0, 20)], [("gg", nr + 16, nr + 336)])
        zq, zs, zt = "zq%d" % r, "zs%d" % r, "zt%d" % r
        pairs(r, 0, 128, range(4))
        for i in range(2):
            nxt = (128, 256) if i == 0 else (CROSS, C)
            pairs(r, nxt[0], nxt[1], [0])
            quant(zq, zs, 128 * i, 128 * i + 128, zt, 512 * i, 512 * i + 512)
            layer(r, 128 * i, 4 * i)
            keep(r, 128 * i, 4 * i)
            pairs(r, nxt[0], nxt[1], [1, 2, 3] if i == 0 else [1, 2])
        ship(r, 0)
        pairs(r, CROSS, C, [3])
        ship(r, 1)
        quant(zq, zs, 256, 384, zt, 4 * 192, 4 * C)
        layer(r, 256, 0)
        for b in range(4):
            act(T["bp%d" % r][:, C * b + CROSS:C * b + C], T.ps[:, 512 * b + 64:512 * b + 128], ACT.Copy,
                [bank(b)], [("bp%d" % r, C * b + CROSS, C * b + C)], scale=0.03125)
        turn("gg", nr, HALF)
        wrapped("kof%d" % (r + 1), 0, 2, 0, 1.0, 160.0)
        if r + 1 < ROUNDS:
            k4 = "k4%d" % (r + 1)
            for t in range(4):
                wrapped(k4, 32 * t, 2, 0, 4.0, 640.0 + t)
            dma("s", "dk%d" % (r + 1), [(T["lk%d" % (r + 1)][:, :], T.gg[0:128:16, nr + 16:nr + 336],
                                         [("gg", nr + 16, nr + 336)], [("lk%d" % (r + 1), 0, 160)])])
            share(r + 1)
            fetch(r + 1)
        else:
            tts(T.kpf[:], T.gg[:, nr + 16:nr + 336], 160.0, None, A.add, None, [("gg", nr + 16, nr + 336)], [("kpf", 0, C)])
            dma("s", "okp", [(T.kp[:, :], T.kpf[0:128:16, :], [("kpf", 0, C)], [])])
            quant("vq", "vs", 0, 128, "vb", 0, 512)
        if r == 0:
            quant("eq", "ep", 0, 512, "eb", 0, 2048)
        unpack(r, 0, 4)
        unpack(r, 1, 0)
        n = r + 1
        advance(r, 0, range(4))
        advance(r, 1, [0])
        if n < ROUNDS:
            qstate(n, 0)
            score(n, 0)
            advance(r, 1, [1, 2, 3])
            qstate(n, 1)
            score(n, 1)
            sign(0)
            sign(1)
        else:
            for i in range(2):
                a, b = PARTS[i]
                if i == 1:
                    advance(r, 1, [1, 2, 3])
                qstate(n, i)
                mul(4 + i, b - a, "vq", "vs", 0, "xq%d" % n, "xs%d" % n, a, b)
                act(T.yo[:, a:b], T.ps[:, 512 * (4 + i):512 * (4 + i) + b - a], ACT.Copy, [bank(4 + i)], [("yo", a, b)])
                dma("s", "oc%d" % i, [(T.oc[:, 4 * a:4 * b], T["xq%d" % n][:, a:b].bitcast(dt.uint8), [("xq%d" % n, a, b)], [])])
                dma("a", "oy%d" % i, [(T.y[:, a:b], T.yo[:, a:b], [("yo", a, b)], [])])
            dma("s", "os", [(T.osc[4 * i:4 * i + 4, :], T["xs%d" % n][32 * i:32 * i + 4, :], [("xs%d" % n, 0, C)], []) for i in range(4)])
    for sem in total:
        if seen["g"].get(sem, 0) < total[sem]:
            g.wait_ge(T.sem[sem], total[sem])
